import numpy as np
import ml_dtypes


def mxq(x, axis, fmt="e4m3"):
    dtype, down = {"e4m3": (ml_dtypes.float8_e4m3fn, 7), "e5m2": (ml_dtypes.float8_e5m2, 14)}[fmt]
    v = np.moveaxis(np.asarray(x, np.float32).astype(ml_dtypes.bfloat16).astype(np.float64), axis, -1)
    blocks = v.reshape(v.shape[:-1] + (-1, 32))
    amax = np.abs(blocks).max(-1, keepdims=True)
    byte = np.maximum(np.where(amax > 0, np.frexp(amax)[1] - 1 + 127, 0) - down, 1)
    scale = np.exp2(byte - 127.0)
    codes = (blocks / scale).astype(np.float32).astype(dtype).astype(np.float64)
    return np.moveaxis((codes * scale).reshape(v.shape), -1, axis)


WIDE = False


def mx_kscale(k):
    if not WIDE:
        return np.ones(k)
    levels = np.array([10, -10, 5, -5, 0])
    if k % 512:
        return np.exp2(np.random.permutation(np.resize(levels, k // 32))).repeat(32)
    a = np.empty((k // 512, 16))
    for p in range(k // 512):
        a[p, :8] = np.random.permutation(np.resize(levels, 8))
        for g in range(8):
            far = levels[np.abs(levels - a[p, g]) >= 10]
            a[p, g + 8] = far[np.random.randint(len(far))]
    return np.exp2(a.ravel()).repeat(32)


BF16 = ml_dtypes.bfloat16


def bf(x):
    return np.asarray(x, np.float32).astype(BF16)


def f64(x):
    return np.asarray(x).astype(np.float64)

E4M3FN = np.array([(-1.0 if i & 128 else 1.0) * ((1.0 + (i & 7) / 8.0) * 2.0 ** (((i >> 3) & 15) - 7) if i & 120 else (i & 7) * 2.0 ** -9) for i in range(256)])


def e4m3fn_bytes(y):
    return np.clip(np.asarray(y, np.float64), -448.0, 448.0).astype(np.float32).astype(ml_dtypes.float8_e4m3fn).view(np.uint8)


def e4m3fn_values(b):
    return E4M3FN[b]


N, K, F, G = 1536, 1024, 512, 128


def setup_inputs():
    s, t = mx_kscale(K), mx_kscale(F)
    z = np.random.standard_normal((N, K)) / K ** 0.25 * s
    d = np.random.standard_normal((F, K)) / np.sqrt(F) / K ** 0.25 / t[:, None]
    z_scale = (np.abs(z).reshape(N, K // G, G).max(axis=2) / 448).astype(np.float32)
    d_scale = (np.abs(d).reshape(F // G, G, K // G, G).max(axis=(1, 3)) / 448).astype(np.float32)
    return {"z_bytes": e4m3fn_bytes(z / np.repeat(f64(z_scale), G, axis=1)),
            "z_scale": z_scale,
            "w": bf(np.random.standard_normal((K, K)) / np.sqrt(K) / s[:, None]),
            "x": bf(np.random.standard_normal((N, F)) * t),
            "d_bytes": e4m3fn_bytes(d / np.repeat(np.repeat(f64(d_scale), G, axis=0), G, axis=1)),
            "d_scale": d_scale,
            "r": bf((1 + 0.1 * np.random.standard_normal(K)) / s),
            "b": bf(0.5 * np.random.standard_normal(N))}


def reference(z_bytes, z_scale, w, x, d_bytes, d_scale, r, b):
    z = e4m3fn_values(z_bytes) * np.repeat(f64(z_scale), G, axis=1)
    d = e4m3fn_values(d_bytes) * np.repeat(np.repeat(f64(d_scale), G, axis=0), G, axis=1)
    zq = mxq(z, 1, "e4m3")
    p = (zq @ mxq(f64(w), 0, "e4m3")) + (mxq(f64(x), 1, "e4m3") @ mxq(d, 0, "e4m3"))
    h = p * f64(r)
    logits = (mxq(h, 1, "e4m3") @ zq.T) + f64(b)
    return 1 / (1 + np.exp(-logits))

@@ -1,0 +1,254 @@
+from contextlib import ExitStack
+
+import concourse.mybir as mybir
+from concourse.masks import make_identity
+
+F32 = mybir.dt.float32
+BF16 = mybir.dt.bfloat16
+U32 = mybir.dt.uint32
+U8 = mybir.dt.uint8
+FP8 = mybir.dt.float8_e4m3fn
+FP8X4 = mybir.dt.float8_e4m3fn_x4
+MULT = mybir.AluOpType.mult
+ADD = mybir.AluOpType.add
+ACT = mybir.ActivationFunctionType
+
+N, K, F = 1536, 1024, 512
+P = 128
+CH = 512
+NCH = N // CH
+FLOPS = 2 * N * K * K + 2 * N * F * K + 2 * N * N * K
+
+LOADS = "zs,z0_0,d0,w0_0,w0_1,x0_0,z0_1,x0_1,z1_0,z1_1,x1_0,x1_1,w1_0,w1_1,d1,z2_0,z2_1,x2_0,x2_1,b"
+ORDER = """
+ZW.0.V ZT.0.T ZW.1.S DW.0.V WI.0.0.V WI.0.1.V ZC.0.S DS.0.S ZT.1.T XT.0.0.T
+ZC.1.V ZW.2.V ZQ.0.0.V WQ.0.V XT.0.1.T XC.0.0.S XQ.0.0.V ZW.3.S ZT.2.T XC.0.1.S
+ZC.2.S ZW.6.S ZT.3.T ZC.3.S DQ.0.V XT.1.1.T ZW.4.S ZW.7.V A.1.0.T XC.1.1.V
+ZQ.0.1.V ZT.6.T XT.1.0.T XQ.0.1.V ZC.6.S A.2.0.T ZT.4.T XC.1.0.S ZT.7.T DW.1.S
+A.3.0.T HT.1.0.V WI.1.1.V XQ.1.1.V ZC.7.S WI.1.0.V A.0.0.T ZC.4.S HT.2.0.V XT.2.0.T
+ZQ.1.1.V DS.1.S XT.2.1.T HT.0.0.V XC.2.1.S HT.3.0.V A.7.0.T WQ.1.V A.6.0.T DQ.1.V
+HT.7.0.V A.6.1.T ZW.9.S HT.6.0.V HQ.3.0.V A.3.1.T A.2.1.T XC.2.0.V HQ.2.0.V ZW.8.S
+HT.6.1.V XQ.2.0.V ZT.8.T HQ.1.0.V HQ.0.0.V ZT.9.T HT.3.1.V HT.2.1.V HQ.6.1.V ZW.5.S
+XQ.1.0.V ZW.11.S HQ.3.1.V ZC.8.S A.7.1.T A.1.1.T HQ.2.1.V ZW.10.S HT.7.1.V XQ.2.1.V
+HQ.6.0.V ZT.5.T ZC.9.V B.2.0.T HQ.7.1.V HT.1.1.V ZT.10.T ZC.5.S ZT.11.T ZC.10.S
+A.0.1.T ZQ.2.0.V A.8.0.T HQ.7.0.V B.7.0.T BA.2.0.V ZQ.1.0.V HT.0.1.V ZC.11.S B.6.0.T
+A.8.1.T HT.8.0.V A.4.1.T ZQ.2.1.V BA.7.0.V BA.6.0.V HQ.0.1.V B.6.2.T HT.4.1.V B.3.2.T
+BA.6.2.V B.2.2.T B.7.1.T HQ.1.1.V BA.3.2.V SG.3.2.S BA.2.2.V A.11.0.T HT.8.1.V HQ.8.0.V
+B.1.0.T B.0.2.T SG.7.0.S BA.7.1.V B.6.1.T A.10.0.T HT.11.0.V BA.1.0.V BA.0.2.V B.0.0.T
+B.0.1.T HQ.4.1.V A.4.0.T SG.7.1.S HT.10.0.V BA.6.1.V SG.2.2.S SG.2.0.S HQ.8.1.V SG.1.0.S
+BA.0.1.V SG.0.1.S A.11.1.T B.8.2.T BA.0.0.V HT.4.0.V SG.0.0.S A.5.1.T HT.11.1.V BA.8.2.V
+SG.6.0.S HQ.11.0.V B.3.1.T HQ.10.0.V B.3.0.T HT.5.1.V B.8.0.T HQ.11.1.V A.10.1.T SG.6.2.S
+BA.3.1.V HQ.4.0.V BA.3.0.V B.7.2.T SG.0.2.S SG.8.2.S BA.8.0.V B.11.2.T HT.10.1.V BA.7.2.V
+A.5.0.T HQ.5.1.V B.8.1.T BA.11.2.V HQ.10.1.V A.9.0.T HT.5.0.V BA.8.1.V SG.6.1.S HQ.5.0.V
+SG.8.0.S B.4.2.T HT.9.0.V BA.4.2.V B.1.1.T SG.7.2.S B.4.0.T BA.1.1.V B.5.0.T SG.3.1.S
+B.11.0.T BA.4.0.V SG.11.2.S A.9.1.T HQ.9.0.V BA.5.0.V BA.11.0.V SG.8.1.S B.10.0.T SG.3.0.S
+HT.9.1.V BA.10.0.V B.4.1.T B.5.2.T BA.4.1.V BA.5.2.V SG.4.2.S HQ.9.1.V SG.4.0.S SG.1.1.S
+SG.5.0.S SG.11.0.S B.10.2.T BA.10.2.V B.11.1.T SG.10.0.S B.2.1.T SG.4.1.S BA.11.1.V BA.2.1.V
+B.5.1.T SG.5.2.S B.9.1.T B.9.0.T SG.10.2.S SG.11.1.S SG.2.1.S BA.5.1.V SG.5.1.S BA.9.1.V
+BA.9.0.V SG.9.1.S B.10.1.T SG.9.0.S BA.10.1.V SG.10.1.S B.1.2.T BA.1.2.V B.9.2.T SG.1.2.S
+BA.9.2.V SG.9.2.S
+"""
+
+
+def tile_bilinear_edge_decoder_d9_kernel(tc, z_bytes, z_scale, w, x, d_bytes, d_scale, r, b, out):
+    nc = tc.nc
+    steps = [(s.split(".")[0], [int(v) for v in s.split(".")[1:-1]], s.split(".")[-1]) for s in ORDER.split()]
+    eng = {}
+    for s in ORDER.split():
+        parts = s.split(".")
+        eng[".".join(parts[:-1])] = parts[-1]
+    with ExitStack() as ctx:
+        keep = ctx.enter_context(tc.tile_pool(name="keep", bufs=1))
+        zwp = ctx.enter_context(tc.tile_pool(name="zwp", bufs=6))
+        two = ctx.enter_context(tc.tile_pool(name="two", bufs=2))
+        lgp = ctx.enter_context(tc.tile_pool(name="lgp", bufs=14))
+        ps_t = ctx.enter_context(tc.psum_pool(name="ps_t", bufs=2))
+        ps_1 = ctx.enter_context(tc.psum_pool(name="ps_1", bufs=3))
+        ps_2 = ctx.enter_context(tc.psum_pool(name="ps_2", bufs=3))
+        ctx.enter_context(tc.manual_schedule())
+
+        zs = keep.tile([P, 12, 8], F32, name="zs")
+        ds = keep.tile([P, 8], F32, name="ds")
+        rt = keep.tile([P, 2, 4], BF16, name="rt")
+        bt = keep.tile([P, N], BF16, name="bt")
+        zb = [keep.tile([P, 4, K], U8, name="zb%d" % c) for c in range(NCH)]
+        xb = [keep.tile([P, 4, F], BF16, name="xb%d" % c) for c in range(NCH)]
+        wr = [[keep.tile([P, 4, 512], BF16, name="wr%d%d" % (h, g)) for g in range(2)] for h in range(2)]
+        db = [keep.tile([P, 4, 512], U8, name="db%d" % h) for h in range(2)]
+
+        dall = keep.tile([P, 32], F32, name="dall")
+        nc.scalar.dma_start(out=dall[:], in_=d_scale.rearrange("a c -> (a c)").partition_broadcast(P))
+        warm = keep.tile([P, 1], F32, name="warm")
+        nc.vector.memset(warm[:], 0.0)
+        nc.scalar.activation(warm[:], warm[:], ACT.Sigmoid)
+        ident = keep.tile([P, P], F32, name="ident")
+        make_identity(nc, ident[:])
+        nc.gpsimd.dma_start(out=rt[:], in_=r.rearrange("(h p t) -> p h t", h=2, p=P))
+        for a in range(4):
+            rows = slice(32 * a, 32 * a + 32)
+            nc.vector.tensor_copy(ds[rows, :], dall[rows, 8 * a:8 * a + 8])
+
+        for ld in LOADS.split(","):
+            if ld == "zs":
+                nc.sync.dma_start(out=zs[:], in_=z_scale.rearrange("(n p) c -> p n c", p=P))
+            elif ld == "b":
+                nc.sync.dma_start(out=bt[:], in_=b.partition_broadcast(P))
+            elif ld[0] == "z":
+                c, i = int(ld[1]), int(ld[3])
+                nc.sync.dma_start(out=zb[c][:, 2 * i:2 * i + 2, :], in_=z_bytes[CH * c + 256 * i:CH * c + 256 * i + 256, :].rearrange("(n p) k -> p n k", p=P))
+            elif ld[0] == "x":
+                c, i = int(ld[1]), int(ld[3])
+                nc.sync.dma_start(out=xb[c][:, 2 * i:2 * i + 2, :], in_=x[CH * c + 256 * i:CH * c + 256 * i + 256, :].rearrange("(n p) f -> p n f", p=P))
+            elif ld[0] == "w":
+                h, g = int(ld[1]), int(ld[3])
+                nc.sync.dma_start(out=wr[h][g][:], in_=w[512 * g:512 * g + 512, 512 * h:512 * h + 512].rearrange("(p j) c -> p j c", j=4))
+            else:
+                h = int(ld[1])
+                nc.sync.dma_start(out=db[h][:], in_=d_bytes[:, 512 * h:512 * h + 512].rearrange("(p j) c -> p j c", j=4))
+
+        zc = [keep.tile([P, 2, CH], U32, name="zc%d" % c, align_bytes=256) for c in range(NCH)]
+        zsc = [keep.tile([P, 2, CH], U8, name="zsc%d" % c, align_bytes=256) for c in range(NCH)]
+        xc = [keep.tile([P, CH], U32, name="xc%d" % c, align_bytes=256) for c in range(NCH)]
+        xsc = [keep.tile([P, CH], U8, name="xsc%d" % c, align_bytes=256) for c in range(NCH)]
+        wc = [keep.tile([P, 2, 512], U32, name="wc%d" % h, align_bytes=256) for h in range(2)]
+        wsc = [keep.tile([P, 2, 512], U8, name="wsc%d" % h, align_bytes=256) for h in range(2)]
+        dc = [keep.tile([P, 512], U32, name="dc%d" % h, align_bytes=256) for h in range(2)]
+        dsc = [keep.tile([P, 512], U8, name="dsc%d" % h, align_bytes=256) for h in range(2)]
+        hc = [keep.tile([P, 2, P], U32, name="hc%d" % n, align_bytes=256) for n in range(12)]
+        hsc = [keep.tile([P, 2, P], U8, name="hsc%d" % n, align_bytes=256) for n in range(12)]
+        zt = [keep.tile([P, 2, 2, 1024], BF16, name="zt%d" % c, align_bytes=64) for c in range(NCH)]
+        xt = [keep.tile([P, 2, 1024], BF16, name="xt%d" % c, align_bytes=64) for c in range(NCH)]
+        wt = [keep.tile([P, 2, 2048], BF16, name="wt%d" % h, align_bytes=64) for h in range(2)]
+        dw = [keep.tile([P, 4, 512], BF16, name="dw%d" % h) for h in range(2)]
+        dt = [keep.tile([P, 2048], BF16, name="dt%d" % h, align_bytes=64) for h in range(2)]
+        st = {}
+
+        def quant(codes, scales, src):
+            nc.vector.quantize_mx(out=codes.bitcast(FP8X4), scales=scales, in_=src)
+
+        def copy(e, dst, src):
+            if e == "V":
+                nc.vector.tensor_copy(dst, src)
+            elif e == "S":
+                nc.scalar.copy(dst, src)
+            else:
+                nc.gpsimd.tensor_scalar(dst, src, 1.0, 0.0, MULT, ADD)
+
+        def do_ZW(e, n):
+            c, i = n // 4, n % 4
+            zw = zwp.tile([P, K], BF16, name="zw", align_bytes=64)
+            st["zw", n] = zw
+            for q in range(8):
+                src = zb[c][:, i, P * q:P * q + P].bitcast(FP8)
+                if e == "V":
+                    g, m = q // 4, 32 * (q % 4)
+                    dst = zw[:].rearrange("P (g u p e) -> P g p u e", g=2, u=2, e=2)[:, g, m:m + 32, :, :]
+                    nc.vector.tensor_scalar(dst, src.rearrange("P (p u e) -> P p u e", u=2, e=2), zs[:, n, q:q + 1], None, MULT)
+                else:
+                    nc.scalar.activation(zw[:, P * q:P * q + P], src, ACT.Copy, scale=zs[:, n, q:q + 1])
+
+        def do_ZT(e, n):
+            words = st["zw", n][:].bitcast(F32)
+            bank = ps_t.tile([P, 4, P], F32, name="tbank")
+            st["zp", n] = bank
+            for g in range(2):
+                for u in range(2):
+                    if eng["ZW.%d" % n] == "V":
+                        src = words[:, 256 * g + 128 * u:256 * g + 128 * u + 128]
+                    else:
+                        src = words[:, 256 * g + u:256 * g + 256:2]
+                    nc.tensor.transpose(bank[:, 2 * g + u, :], src, ident[:])
+
+        def do_ZC(e, n):
+            c, i = n // 4, n % 4
+            dst = zt[c][:, i // 2, :, :].bitcast(F32).rearrange("p g (r u) -> p g r u", u=2)[:, :, P * (i % 2):P * (i % 2) + P, :]
+            copy(e, dst, st["zp", n][:].rearrange("p (g u) r -> p g r u", g=2))
+
+        def do_ZQ(e, c, m):
+            for g in range(2):
+                quant(zc[c][:, g, 256 * m:256 * m + 256], zsc[c][:, g, 256 * m:256 * m + 256], zt[c][:, m, g, :])
+
+        def do_XT(e, c, m):
+            bank = ps_t.tile([P, 4, P], F32, name="tbank")
+            st["xp", c, m] = bank
+            for i in range(2):
+                words = xb[c][:, 2 * m + i, :].bitcast(F32)
+                for u in range(2):
+                    nc.tensor.transpose(bank[:, 2 * i + u, :], words[:, u:256:2], ident[:])
+
+        def do_XC(e, c, m):
+            dst = xt[c][:, m, :].bitcast(F32).rearrange("p (i r u) -> p i r u", i=2, u=2)
+            copy(e, dst, st["xp", c, m][:].rearrange("p (i u) r -> p i r u", u=2))
+
+        def do_XQ(e, c, m):
+            quant(xc[c][:, 256 * m:256 * m + 256], xsc[c][:, 256 * m:256 * m + 256], xt[c][:, m, :])
+
+        def do_WI(e, h, g):
+            copy(e, wt[h][:, g, :].rearrange("p (t m j) -> p t m j", t=4, j=4), wr[h][g][:].rearrange("p j (m t) -> p t m j", t=4))
+
+        def do_WQ(e, h):
+            quant(wc[h][:].rearrange("p g n -> p (g n)"), wsc[h][:].rearrange("p g n -> p (g n)"), wt[h][:].rearrange("p g n -> p (g n)"))
+
+        def do_DW(e, h):
+            dst = dw[h][:].rearrange("p j c -> p (j c)")
+            src = db[h][:].rearrange("p j c -> p (j c)").bitcast(FP8)
+            if e == "V":
+                nc.vector.tensor_copy(dst, src)
+            elif e == "S":
+                nc.scalar.copy(dst, src)
+            else:
+                nc.gpsimd.tensor_copy(dst, src)
+
+        def do_DS(e, h):
+            for q in range(4):
+                dst = dt[h][:].rearrange("p (t m j) -> p t m j", t=4, j=4)[:, :, 32 * q:32 * q + 32, :]
+                src = dw[h][:].rearrange("p j (m t) -> p t m j", t=4)[:, :, 32 * q:32 * q + 32, :]
+                sc = ds[:, 4 * h + q:4 * h + q + 1]
+                if e == "V":
+                    nc.vector.tensor_scalar(dst, src, sc, None, MULT)
+                elif e == "S":
+                    nc.scalar.activation(dst, src, ACT.Copy, scale=sc)
+                else:
+                    nc.gpsimd.tensor_scalar(dst, src, sc, 0.0, MULT, ADD)
+
+        def do_DQ(e, h):
+            quant(dc[h][:], dsc[h][:], dt[h][:])
+
+        def do_A(e, n, h):
+            c, i = n // 4, n % 4
+            cols = slice(P * i, P * i + P)
+            bank = ps_1.tile([P, 4, P], F32, name="hbank")
+            st["hp", n, h] = bank
+            for t in range(4):
+                s4 = slice(P * t, P * t + P)
+                for g in range(2):
+                    nc.tensor.matmul_mx(out=bank[:, t, :], lhsT=wc[h][:, g, s4].bitcast(FP8X4), lhsT_scale=wsc[h][:, g, s4], rhs=zc[c][:, g, cols].bitcast(FP8X4), rhs_scale=zsc[c][:, g, cols], start=(g == 0), stop=False)
+                nc.tensor.matmul_mx(out=bank[:, t, :], lhsT=dc[h][:, s4].bitcast(FP8X4), lhsT_scale=dsc[h][:, s4], rhs=xc[c][:, cols].bitcast(FP8X4), rhs_scale=xsc[c][:, cols], start=False, stop=True)
+
+        def do_HT(e, n, h):
+            ht = two.tile([P, P, 4], BF16, name="ht", align_bytes=64, bufs=12)
+            st["ht", n, h] = ht
+            nc.vector.tensor_tensor(ht[:], st["hp", n, h][:].rearrange("p t n -> p n t"), rt[:, h, :].unsqueeze(1).to_broadcast([P, P, 4]), MULT)
+
+        def do_HQ(e, n, h):
+            quant(hc[n][:, h, :], hsc[n][:, h, :], st["ht", n, h][:].rearrange("p n t -> p (n t)"))
+
+        def do_B(e, n, c):
+            bank = ps_2.tile([P, CH], F32, name="obank")
+            st["op", n, c] = bank
+            for g in range(2):
+                nc.tensor.matmul_mx(out=bank[:], lhsT=hc[n][:, g, :].bitcast(FP8X4), lhsT_scale=hsc[n][:, g, :], rhs=zc[c][:, g, :].bitcast(FP8X4), rhs_scale=zsc[c][:, g, :], start=(g == 0), stop=(g == 1))
+
+        def do_BA(e, n, c):
+            lg = lgp.tile([P, CH], F32, name="lg")
+            st["lg", n, c] = lg
+            nc.vector.tensor_tensor(lg[:], st["op", n, c][:], bt[:, CH * c:CH * c + CH], ADD)
+
+        def do_SG(e, n, c):
+            og = st["lg", n, c]
+            nc.scalar.activation(og[:], og[:], ACT.Sigmoid)
+            nc.sync.dma_start(out=out[P * n:P * n + P, CH * c:CH * c + CH], in_=og[:])
+
+        table = dict(ZW=do_ZW, ZT=do_ZT, ZC=do_ZC, ZQ=do_ZQ, XT=do_XT, XC=do_XC, XQ=do_XQ, WI=do_WI, WQ=do_WQ, DW=do_DW, DS=do_DS, DQ=do_DQ, A=do_A, HT=do_HT, HQ=do_HQ, B=do_B, BA=do_BA, SG=do_SG)
+        for kind, args, e in steps:
+            table[kind](e, *args)

@@ -19,34 +19,34 @@ CH = 512
 NCH = N // CH
 FLOPS = 2 * N * K * K + 2 * N * F * K + 2 * N * N * K
 
-LOADS = "zs,z0_0,d0,w0_0,w0_1,x0_0,z0_1,x0_1,z1_0,z1_1,x1_0,x1_1,w1_0,w1_1,d1,z2_0,z2_1,x2_0,x2_1,b"
+LOADS = "zs,z0_0,d0,w0_0,w0_1,x0_0,z0_1,x0_1,w1_0,w1_1,d1,z1_0,z1_1,x1_0,x1_1,z2_0,z2_1,x2_0,x2_1,b"
 ORDER = """
-ZW.0.V ZT.0.T ZW.1.S DW.0.V WI.0.0.V WI.0.1.V ZC.0.S DS.0.S ZT.1.T XT.0.0.T
-ZC.1.V ZW.2.V ZQ.0.0.V WQ.0.V XT.0.1.T XC.0.0.S XQ.0.0.V ZW.3.S ZT.2.T XC.0.1.S
-ZC.2.S ZW.6.S ZT.3.T ZC.3.S DQ.0.V XT.1.1.T ZW.4.S ZW.7.V A.1.0.T XC.1.1.V
-ZQ.0.1.V ZT.6.T XT.1.0.T XQ.0.1.V ZC.6.S A.2.0.T ZT.4.T XC.1.0.S ZT.7.T DW.1.S
-A.3.0.T HT.1.0.V WI.1.1.V XQ.1.1.V ZC.7.S WI.1.0.V A.0.0.T ZC.4.S HT.2.0.V XT.2.0.T
-ZQ.1.1.V DS.1.S XT.2.1.T HT.0.0.V XC.2.1.S HT.3.0.V A.7.0.T WQ.1.V A.6.0.T DQ.1.V
-HT.7.0.V A.6.1.T ZW.9.S HT.6.0.V HQ.3.0.V A.3.1.T A.2.1.T XC.2.0.V HQ.2.0.V ZW.8.S
-HT.6.1.V XQ.2.0.V ZT.8.T HQ.1.0.V HQ.0.0.V ZT.9.T HT.3.1.V HT.2.1.V HQ.6.1.V ZW.5.S
-XQ.1.0.V ZW.11.S HQ.3.1.V ZC.8.S A.7.1.T A.1.1.T HQ.2.1.V ZW.10.S HT.7.1.V XQ.2.1.V
-HQ.6.0.V ZT.5.T ZC.9.V B.2.0.T HQ.7.1.V HT.1.1.V ZT.10.T ZC.5.S ZT.11.T ZC.10.S
-A.0.1.T ZQ.2.0.V A.8.0.T HQ.7.0.V B.7.0.T BA.2.0.V ZQ.1.0.V HT.0.1.V ZC.11.S B.6.0.T
-A.8.1.T HT.8.0.V A.4.1.T ZQ.2.1.V BA.7.0.V BA.6.0.V HQ.0.1.V B.6.2.T HT.4.1.V B.3.2.T
-BA.6.2.V B.2.2.T B.7.1.T HQ.1.1.V BA.3.2.V SG.3.2.S BA.2.2.V A.11.0.T HT.8.1.V HQ.8.0.V
-B.1.0.T B.0.2.T SG.7.0.S BA.7.1.V B.6.1.T A.10.0.T HT.11.0.V BA.1.0.V BA.0.2.V B.0.0.T
-B.0.1.T HQ.4.1.V A.4.0.T SG.7.1.S HT.10.0.V BA.6.1.V SG.2.2.S SG.2.0.S HQ.8.1.V SG.1.0.S
-BA.0.1.V SG.0.1.S A.11.1.T B.8.2.T BA.0.0.V HT.4.0.V SG.0.0.S A.5.1.T HT.11.1.V BA.8.2.V
-SG.6.0.S HQ.11.0.V B.3.1.T HQ.10.0.V B.3.0.T HT.5.1.V B.8.0.T HQ.11.1.V A.10.1.T SG.6.2.S
-BA.3.1.V HQ.4.0.V BA.3.0.V B.7.2.T SG.0.2.S SG.8.2.S BA.8.0.V B.11.2.T HT.10.1.V BA.7.2.V
-A.5.0.T HQ.5.1.V B.8.1.T BA.11.2.V HQ.10.1.V A.9.0.T HT.5.0.V BA.8.1.V SG.6.1.S HQ.5.0.V
-SG.8.0.S B.4.2.T HT.9.0.V BA.4.2.V B.1.1.T SG.7.2.S B.4.0.T BA.1.1.V B.5.0.T SG.3.1.S
-B.11.0.T BA.4.0.V SG.11.2.S A.9.1.T HQ.9.0.V BA.5.0.V BA.11.0.V SG.8.1.S B.10.0.T SG.3.0.S
-HT.9.1.V BA.10.0.V B.4.1.T B.5.2.T BA.4.1.V BA.5.2.V SG.4.2.S HQ.9.1.V SG.4.0.S SG.1.1.S
-SG.5.0.S SG.11.0.S B.10.2.T BA.10.2.V B.11.1.T SG.10.0.S B.2.1.T SG.4.1.S BA.11.1.V BA.2.1.V
-B.5.1.T SG.5.2.S B.9.1.T B.9.0.T SG.10.2.S SG.11.1.S SG.2.1.S BA.5.1.V SG.5.1.S BA.9.1.V
-BA.9.0.V SG.9.1.S B.10.1.T SG.9.0.S BA.10.1.V SG.10.1.S B.1.2.T BA.1.2.V B.9.2.T SG.1.2.S
-BA.9.2.V SG.9.2.S
+ZW.1.V ZT.1.T DW.0.V WI.0.0.V ZW.0.S ZC.1.S WI.0.1.V DS.0.S ZW.3.V XT.0.0.T
+DQ.0.V ZT.0.T XC.0.0.S XT.0.1.T ZW.2.S ZC.0.S ZT.3.T XC.0.1.S WQ.0.V XQ.0.0.V
+ZT.2.T ZQ.0.0.V AQ.0.0.0.1.T ZC.3.S AQ.0.0.0.0.T WI.1.0.V ZC.2.S ZW.5.V ZT.5.T XT.1.0.T
+ZQ.0.1.V XQ.0.1.V HE.0.0.0.1.V AQ.0.1.0.1.T DW.1.S ZC.5.S XC.1.0.V DS.1.S XT.1.1.T XT.2.1.T
+WI.1.1.V ZW.6.V WQ.1.V DQ.1.V XC.1.1.S XC.2.1.S AQ.0.1.0.0.T HE.0.0.0.0.S XT.2.0.T ZT.6.T
+XC.2.0.S AQ.0.0.1.1.T ZW.9.V ZT.9.T ZC.6.S ZW.7.V XQ.1.0.V ZT.7.T HE.0.1.0.1.S XQ.1.1.V
+HI.0.0.0.V AQ.0.1.1.0.T HE.0.1.0.0.S HE.0.0.1.1.S ZC.9.S AQ.0.0.1.0.T ZW.11.V ZW.4.V ZC.7.S HE.0.0.1.0.S
+HE.0.1.1.0.V AQ.0.1.1.1.T HE.0.1.1.1.S ZQ.1.1.V HI.0.0.1.V ZT.4.T ZW.8.V HR.0.0.1.V HR.0.0.0.V ZT.11.T
+ZC.11.S ZC.4.S AQ.1.1.0.0.T HI.0.1.1.V AQ.1.1.0.1.T ZQ.1.0.V HE.1.1.0.0.S ZW.10.S AQ.1.1.1.0.T HI.0.1.0.V
+AQ.1.1.1.1.T B.0.1.T HE.1.1.1.0.S ZT.8.T XQ.2.0.V ZT.10.T HR.0.1.0.V HE.1.1.0.1.S BA.0.1.V B.0.0.T
+B.1.0.T ZC.8.S AQ.1.0.1.0.T ZC.10.S HI.1.1.0.V ZQ.2.0.V HR.0.1.1.V BA.1.0.V ZQ.2.1.V HE.1.1.1.1.S
+SG.1.0.S HR.1.1.0.V AQ.2.0.1.0.T AQ.2.0.1.1.T B.3.2.T BA.0.0.V HE.2.0.1.1.V HE.1.0.1.0.S XQ.2.1.V BA.3.2.V
+B.2.2.T HE.2.0.1.0.S SG.3.2.S B.3.1.T AQ.2.0.0.0.T HE.2.0.0.0.S BA.2.2.V AQ.1.0.1.1.T AQ.2.0.0.1.T HE.1.0.1.1.S
+BA.3.1.V HI.1.1.1.V HR.1.1.1.V HE.2.0.0.1.S HI.2.0.1.V B.3.0.T B.7.0.T B.6.2.T SG.0.1.S SG.3.1.S
+HI.1.0.1.V BA.3.0.V AQ.1.0.0.1.T HI.2.0.0.V AQ.2.1.0.0.T HR.2.0.1.V BA.7.0.V HE.1.0.0.1.S SG.2.2.S HR.2.0.0.V
+BA.6.2.V SG.3.0.S B.2.0.T B.8.2.T SG.6.2.S B.0.2.T BA.2.0.V B.1.1.T SG.0.0.S BA.8.2.V
+SG.2.0.S B.9.0.T SG.7.0.S BA.0.2.V AQ.2.1.0.1.T BA.1.1.V SG.0.2.S HR.1.0.1.V BA.9.0.V B.9.2.T
+HE.2.1.0.0.V HE.2.1.0.1.S SG.1.1.S B.1.2.T BA.9.2.V BA.1.2.V HI.2.1.0.V SG.8.2.S SG.9.2.S B.6.0.T
+AQ.1.0.0.0.T HE.1.0.0.0.S BA.6.0.V B.7.1.T B.7.2.T AQ.2.1.1.0.T SG.1.2.S SG.9.0.S BA.7.1.V SG.7.1.S
+HI.1.0.0.V SG.6.0.S HR.1.0.0.V HE.2.1.1.0.S B.9.1.T BA.7.2.V HR.2.1.0.V BA.9.1.V B.8.0.T AQ.2.1.1.1.T
+SG.7.2.S B.5.1.T HE.2.1.1.1.S B.5.2.T BA.8.0.V BA.5.1.V BA.5.2.V B.4.1.T SG.8.0.S HI.2.1.1.V
+B.6.1.T B.5.0.T BA.4.1.V HR.2.1.1.V BA.6.1.V B.10.2.T B.4.0.T BA.5.0.V BA.10.2.V SG.9.1.S
+SG.5.2.S B.11.2.T B.10.0.T BA.4.0.V BA.11.2.V B.11.1.T SG.5.1.S SG.4.1.S SG.6.1.S BA.10.0.V
+SG.5.0.S BA.11.1.V B.4.2.T BA.4.2.V SG.10.2.S B.10.1.T SG.4.0.S SG.11.2.S B.2.1.T SG.10.0.S
+BA.10.1.V B.11.0.T BA.2.1.V SG.11.1.S SG.4.2.S SG.10.1.S BA.11.0.V SG.2.1.S B.8.1.T SG.11.0.S
+BA.8.1.V SG.8.1.S
 """
 
 
@@ -87,6 +87,8 @@ def tile_bilinear_edge_decoder_d9_kernel(tc, z_bytes, z_scale, w, x, d_bytes, d_
         for a in range(4):
             rows = slice(32 * a, 32 * a + 32)
             nc.vector.tensor_copy(ds[rows, :], dall[rows, 8 * a:8 * a + 8])
+        rf = keep.tile([P, 8], F32, name="rf")
+        nc.gpsimd.tensor_copy(rf[:], rt[:].rearrange("p h t -> p (h t)"))
 
         for ld in LOADS.split(","):
             if ld == "zs":
@@ -114,8 +116,8 @@ def tile_bilinear_edge_decoder_d9_kernel(tc, z_bytes, z_scale, w, x, d_bytes, d_
         wsc = [keep.tile([P, 2, 512], U8, name="wsc%d" % h, align_bytes=256) for h in range(2)]
         dc = [keep.tile([P, 512], U32, name="dc%d" % h, align_bytes=256) for h in range(2)]
         dsc = [keep.tile([P, 512], U8, name="dsc%d" % h, align_bytes=256) for h in range(2)]
-        hc = [keep.tile([P, 2, P], U32, name="hc%d" % n, align_bytes=256) for n in range(12)]
-        hsc = [keep.tile([P, 2, P], U8, name="hsc%d" % n, align_bytes=256) for n in range(12)]
+        hc = [[keep.tile([P, 2, 256], U32, name="hc%d%d" % (c, m), align_bytes=256) for m in range(2)] for c in range(NCH)]
+        hsc = [[keep.tile([P, 2, 256], U8, name="hsc%d%d" % (c, m), align_bytes=256) for m in range(2)] for c in range(NCH)]
         zt = [keep.tile([P, 2, 2, 1024], BF16, name="zt%d" % c, align_bytes=64) for c in range(NCH)]
         xt = [keep.tile([P, 2, 1024], BF16, name="xt%d" % c, align_bytes=64) for c in range(NCH)]
         wt = [keep.tile([P, 2, 2048], BF16, name="wt%d" % h, align_bytes=64) for h in range(2)]
@@ -214,30 +216,46 @@ def tile_bilinear_edge_decoder_d9_kernel(tc, z_bytes, z_scale, w, x, d_bytes, d_
         def do_DQ(e, h):
             quant(dc[h][:], dsc[h][:], dt[h][:])
 
-        def do_A(e, n, h):
-            c, i = n // 4, n % 4
-            cols = slice(P * i, P * i + P)
-            bank = ps_1.tile([P, 4, P], F32, name="hbank")
-            st["hp", n, h] = bank
-            for t in range(4):
+        def do_AQ(e, c, m, h, tp):
+            cols = slice(256 * m, 256 * m + 256)
+            bank = ps_1.tile([P, 2, 256], F32, name="hbank")
+            st["hp", c, m, h, tp] = bank
+            for i in range(2):
+                t = 2 * tp + i
                 s4 = slice(P * t, P * t + P)
                 for g in range(2):
-                    nc.tensor.matmul_mx(out=bank[:, t, :], lhsT=wc[h][:, g, s4].bitcast(FP8X4), lhsT_scale=wsc[h][:, g, s4], rhs=zc[c][:, g, cols].bitcast(FP8X4), rhs_scale=zsc[c][:, g, cols], start=(g == 0), stop=False)
-                nc.tensor.matmul_mx(out=bank[:, t, :], lhsT=dc[h][:, s4].bitcast(FP8X4), lhsT_scale=dsc[h][:, s4], rhs=xc[c][:, cols].bitcast(FP8X4), rhs_scale=xsc[c][:, cols], start=False, stop=True)
+                    nc.tensor.matmul_mx(out=bank[:, i, :], lhsT=wc[h][:, g, s4].bitcast(FP8X4), lhsT_scale=wsc[h][:, g, s4], rhs=zc[c][:, g, cols].bitcast(FP8X4), rhs_scale=zsc[c][:, g, cols], start=(g == 0), stop=False)
+                nc.tensor.matmul_mx(out=bank[:, i, :], lhsT=dc[h][:, s4].bitcast(FP8X4), lhsT_scale=dsc[h][:, s4], rhs=xc[c][:, cols].bitcast(FP8X4), rhs_scale=xsc[c][:, cols], start=False, stop=True)
 
-        def do_HT(e, n, h):
-            ht = two.tile([P, P, 4], BF16, name="ht", align_bytes=64, bufs=12)
-            st["ht", n, h] = ht
-            nc.vector.tensor_tensor(ht[:], st["hp", n, h][:].rearrange("p t n -> p n t"), rt[:, h, :].unsqueeze(1).to_broadcast([P, P, 4]), MULT)
+        def do_HE(e, c, m, h, tp):
+            if ("hpl", c, m, h) not in st:
+                hpl = two.tile([P, 4, 256], BF16, name="hpl", bufs=4)
+                st["hpl", c, m, h] = hpl
+            for i in range(2):
+                t = 2 * tp + i
+                dst = st["hpl", c, m, h][:, t, :]
+                src = st["hp", c, m, h, tp][:, i, :]
+                sc = rf[:, 4 * h + t:4 * h + t + 1]
+                if e == "V":
+                    nc.vector.tensor_scalar(dst, src, sc, None, MULT)
+                else:
+                    nc.scalar.activation(dst, src, ACT.Copy, scale=sc)
 
-        def do_HQ(e, n, h):
-            quant(hc[n][:, h, :], hsc[n][:, h, :], st["ht", n, h][:].rearrange("p n t -> p (n t)"))
+        def do_HI(e, c, m, h):
+            ht = two.tile([P, 256, 4], BF16, name="ht", align_bytes=64, bufs=6)
+            st["ht", c, m, h] = ht
+            copy(e, ht[:], st["hpl", c, m, h][:].rearrange("p t n -> p n t"))
+
+        def do_HR(e, c, m, h):
+            quant(hc[c][m][:, h, :], hsc[c][m][:, h, :], st["ht", c, m, h][:].rearrange("p n t -> p (n t)"))
 
         def do_B(e, n, c):
             bank = ps_2.tile([P, CH], F32, name="obank")
             st["op", n, c] = bank
             for g in range(2):
-                nc.tensor.matmul_mx(out=bank[:], lhsT=hc[n][:, g, :].bitcast(FP8X4), lhsT_scale=hsc[n][:, g, :], rhs=zc[c][:, g, :].bitcast(FP8X4), rhs_scale=zsc[c][:, g, :], start=(g == 0), stop=(g == 1))
+                rows = slice(P * (n % 2), P * (n % 2) + P)
+                hq, hs = hc[n // 4][n % 4 // 2], hsc[n // 4][n % 4 // 2]
+                nc.tensor.matmul_mx(out=bank[:], lhsT=hq[:, g, rows].bitcast(FP8X4), lhsT_scale=hs[:, g, rows], rhs=zc[c][:, g, :].bitcast(FP8X4), rhs_scale=zsc[c][:, g, :], start=(g == 0), stop=(g == 1))
 
         def do_BA(e, n, c):
             lg = lgp.tile([P, CH], F32, name="lg")
@@ -249,6 +267,6 @@ def tile_bilinear_edge_decoder_d9_kernel(tc, z_bytes, z_scale, w, x, d_bytes, d_
             nc.scalar.activation(og[:], og[:], ACT.Sigmoid)
             nc.sync.dma_start(out=out[P * n:P * n + P, CH * c:CH * c + CH], in_=og[:])
 
-        table = dict(ZW=do_ZW, ZT=do_ZT, ZC=do_ZC, ZQ=do_ZQ, XT=do_XT, XC=do_XC, XQ=do_XQ, WI=do_WI, WQ=do_WQ, DW=do_DW, DS=do_DS, DQ=do_DQ, A=do_A, HT=do_HT, HQ=do_HQ, B=do_B, BA=do_BA, SG=do_SG)
+        table = dict(ZW=do_ZW, ZT=do_ZT, ZC=do_ZC, ZQ=do_ZQ, XT=do_XT, XC=do_XC, XQ=do_XQ, WI=do_WI, WQ=do_WQ, DW=do_DW, DS=do_DS, DQ=do_DQ, AQ=do_AQ, HE=do_HE, HI=do_HI, HR=do_HR, B=do_B, BA=do_BA, SG=do_SG)
         for kind, args, e in steps:
             table[kind](e, *args)

@@ -19,7 +19,7 @@ CH = 512
 NCH = N // CH
 FLOPS = 2 * N * K * K + 2 * N * F * K + 2 * N * N * K
 
-LOADS = "zs,z0_0,d0,w0_0,w0_1,x0_0,z0_1,x0_1,w1_0,w1_1,d1,z1_0,z1_1,x1_0,x1_1,z2_0,z2_1,x2_0,x2_1,b"
+LOADS = "zs,z0_0,dr,d0,w0_0,w0_1,x0_0,zr,z0_1,x0_1,w1_0,w1_1,d1,z1_0,z1_1,x1_0,x1_1,z2_0,z2_1,x2_0,x2_1,b"
 ORDER = """
 ZW.1.V ZT.1.T DW.0.V WI.0.0.V ZW.0.S ZC.1.S WI.0.1.V DS.0.S ZW.3.V XT.0.0.T
 DQ.0.V ZT.0.T XC.0.0.S XT.0.1.T ZW.2.S ZC.0.S ZT.3.T XC.0.1.S WQ.0.V XQ.0.0.V
@@ -76,23 +76,28 @@ def tile_bilinear_edge_decoder_d9_kernel(tc, z_bytes, z_scale, w, x, d_bytes, d_
         wr = [[keep.tile([P, 4, 512], BF16, name="wr%d%d" % (h, g)) for g in range(2)] for h in range(2)]
         db = [keep.tile([P, 4, 512], U8, name="db%d" % h) for h in range(2)]
 
-        dall = keep.tile([P, 32], F32, name="dall")
-        nc.scalar.dma_start(out=dall[:], in_=d_scale.rearrange("a c -> (a c)").partition_broadcast(P))
+        drow = keep.tile([P, 8], F32, name="drow")
+        sel = keep.tile([P, P], F32, name="sel")
+        nc.vector.memset(drow[:], 0.0)
+        nc.vector.memset(sel[:], 0.0)
+        for a in range(4):
+            nc.vector.memset(sel[32 * a:32 * a + 1, 32 * a:32 * a + 32], 1.0)
         warm = keep.tile([P, 1], F32, name="warm")
         nc.vector.memset(warm[:], 0.0)
         nc.scalar.activation(warm[:], warm[:], ACT.Sigmoid)
         ident = keep.tile([P, P], F32, name="ident")
         make_identity(nc, ident[:])
         nc.gpsimd.dma_start(out=rt[:], in_=r.rearrange("(h p t) -> p h t", h=2, p=P))
-        for a in range(4):
-            rows = slice(32 * a, 32 * a + 32)
-            nc.vector.tensor_copy(ds[rows, :], dall[rows, 8 * a:8 * a + 8])
         rf = keep.tile([P, 8], F32, name="rf")
         nc.gpsimd.tensor_copy(rf[:], rt[:].rearrange("p h t -> p (h t)"))
 
         for ld in LOADS.split(","):
             if ld == "zs":
-                nc.sync.dma_start(out=zs[:], in_=z_scale.rearrange("(n p) c -> p n c", p=P))
+                nc.sync.dma_start(out=zs[:, 0:4, :], in_=z_scale[0:CH, :].rearrange("(n p) c -> p n c", p=P))
+            elif ld == "zr":
+                nc.sync.dma_start(out=zs[:, 4:12, :], in_=z_scale[CH:N, :].rearrange("(n p) c -> p n c", p=P))
+            elif ld == "dr":
+                nc.sync.dma_start(out=drow[0:P:32, :], in_=d_scale)
             elif ld == "b":
                 nc.sync.dma_start(out=bt[:], in_=b.partition_broadcast(P))
             elif ld[0] == "z":
@@ -186,7 +191,7 @@ def tile_bilinear_edge_decoder_d9_kernel(tc, z_bytes, z_scale, w, x, d_bytes, d_
             quant(xc[c][:, 256 * m:256 * m + 256], xsc[c][:, 256 * m:256 * m + 256], xt[c][:, m, :])
 
         def do_WI(e, h, g):
-            copy(e, wt[h][:, g, :].rearrange("p (t m j) -> p t m j", t=4, j=4), wr[h][g][:].rearrange("p j (m t) -> p t m j", t=4))
+            copy(e, wt[h][:, g, :].rearrange("p (t m j) -> p m t j", t=4, j=4), wr[h][g][:].rearrange("p j (m t) -> p m t j", t=4))
 
         def do_WQ(e, h):
             quant(wc[h][:].rearrange("p g n -> p (g n)"), wsc[h][:].rearrange("p g n -> p (g n)"), wt[h][:].rearrange("p g n -> p (g n)"))
@@ -202,9 +207,13 @@ def tile_bilinear_edge_decoder_d9_kernel(tc, z_bytes, z_scale, w, x, d_bytes, d_
                 nc.gpsimd.tensor_copy(dst, src)
 
         def do_DS(e, h):
+            if h == 0:
+                sbank = ps_t.tile([P, 4, P], F32, name="tbank")
+                nc.tensor.matmul(sbank[:, 0, 0:8], lhsT=sel[:], rhs=drow[:], start=True, stop=True)
+                copy(e, ds[:], sbank[:, 0, 0:8])
             for q in range(4):
-                dst = dt[h][:].rearrange("p (t m j) -> p t m j", t=4, j=4)[:, :, 32 * q:32 * q + 32, :]
-                src = dw[h][:].rearrange("p j (m t) -> p t m j", t=4)[:, :, 32 * q:32 * q + 32, :]
+                dst = dt[h][:].rearrange("p (t m j) -> p m t j", t=4, j=4)[:, 32 * q:32 * q + 32, :, :]
+                src = dw[h][:].rearrange("p j (m t) -> p m t j", t=4)[:, 32 * q:32 * q + 32, :, :]
                 sc = ds[:, 4 * h + q:4 * h + q + 1]
                 if e == "V":
                     nc.vector.tensor_scalar(dst, src, sc, None, MULT)

@@ -15,267 +15,422 @@ ACT = mybir.ActivationFunctionType
 
 N, K, F = 1536, 1024, 512
 P = 128
-CH = 512
-NCH = N // CH
+PASS = 512
+TILE = 128
+HALF = 256
+BLOCK = 512
+TILES, HALVES, BLOCKS = N // TILE, N // HALF, N // BLOCK
 FLOPS = 2 * N * K * K + 2 * N * F * K + 2 * N * N * K
-
-LOADS = "zs,z0_0,dr,d0,w0_0,w0_1,x0_0,zr,z0_1,x0_1,w1_0,w1_1,d1,z1_0,z1_1,x1_0,x1_1,z2_0,z2_1,x2_0,x2_1,b"
-ORDER = """
-ZW.1.V ZT.1.T DW.0.V WI.0.0.V ZW.0.S ZC.1.S WI.0.1.V DS.0.S ZW.3.V XT.0.0.T
-DQ.0.V ZT.0.T XC.0.0.S XT.0.1.T ZW.2.S ZC.0.S ZT.3.T XC.0.1.S WQ.0.V XQ.0.0.V
-ZT.2.T ZQ.0.0.V AQ.0.0.0.1.T ZC.3.S AQ.0.0.0.0.T WI.1.0.V ZC.2.S ZW.5.V ZT.5.T XT.1.0.T
-ZQ.0.1.V XQ.0.1.V HE.0.0.0.1.V AQ.0.1.0.1.T DW.1.S ZC.5.S XC.1.0.V DS.1.S XT.1.1.T XT.2.1.T
-WI.1.1.V ZW.6.V WQ.1.V DQ.1.V XC.1.1.S XC.2.1.S AQ.0.1.0.0.T HE.0.0.0.0.S XT.2.0.T ZT.6.T
-XC.2.0.S AQ.0.0.1.1.T ZW.9.V ZT.9.T ZC.6.S ZW.7.V XQ.1.0.V ZT.7.T HE.0.1.0.1.S XQ.1.1.V
-HI.0.0.0.V AQ.0.1.1.0.T HE.0.1.0.0.S HE.0.0.1.1.S ZC.9.S AQ.0.0.1.0.T ZW.11.V ZW.4.V ZC.7.S HE.0.0.1.0.S
-HE.0.1.1.0.V AQ.0.1.1.1.T HE.0.1.1.1.S ZQ.1.1.V HI.0.0.1.V ZT.4.T ZW.8.V HR.0.0.1.V HR.0.0.0.V ZT.11.T
-ZC.11.S ZC.4.S AQ.1.1.0.0.T HI.0.1.1.V AQ.1.1.0.1.T ZQ.1.0.V HE.1.1.0.0.S ZW.10.S AQ.1.1.1.0.T HI.0.1.0.V
-AQ.1.1.1.1.T B.0.1.T HE.1.1.1.0.S ZT.8.T XQ.2.0.V ZT.10.T HR.0.1.0.V HE.1.1.0.1.S BA.0.1.V B.0.0.T
-B.1.0.T ZC.8.S AQ.1.0.1.0.T ZC.10.S HI.1.1.0.V ZQ.2.0.V HR.0.1.1.V BA.1.0.V ZQ.2.1.V HE.1.1.1.1.S
-SG.1.0.S HR.1.1.0.V AQ.2.0.1.0.T AQ.2.0.1.1.T B.3.2.T BA.0.0.V HE.2.0.1.1.V HE.1.0.1.0.S XQ.2.1.V BA.3.2.V
-B.2.2.T HE.2.0.1.0.S SG.3.2.S B.3.1.T AQ.2.0.0.0.T HE.2.0.0.0.S BA.2.2.V AQ.1.0.1.1.T AQ.2.0.0.1.T HE.1.0.1.1.S
-BA.3.1.V HI.1.1.1.V HR.1.1.1.V HE.2.0.0.1.S HI.2.0.1.V B.3.0.T B.7.0.T B.6.2.T SG.0.1.S SG.3.1.S
-HI.1.0.1.V BA.3.0.V AQ.1.0.0.1.T HI.2.0.0.V AQ.2.1.0.0.T HR.2.0.1.V BA.7.0.V HE.1.0.0.1.S SG.2.2.S HR.2.0.0.V
-BA.6.2.V SG.3.0.S B.2.0.T B.8.2.T SG.6.2.S B.0.2.T BA.2.0.V B.1.1.T SG.0.0.S BA.8.2.V
-SG.2.0.S B.9.0.T SG.7.0.S BA.0.2.V AQ.2.1.0.1.T BA.1.1.V SG.0.2.S HR.1.0.1.V BA.9.0.V B.9.2.T
-HE.2.1.0.0.V HE.2.1.0.1.S SG.1.1.S B.1.2.T BA.9.2.V BA.1.2.V HI.2.1.0.V SG.8.2.S SG.9.2.S B.6.0.T
-AQ.1.0.0.0.T HE.1.0.0.0.S BA.6.0.V B.7.1.T B.7.2.T AQ.2.1.1.0.T SG.1.2.S SG.9.0.S BA.7.1.V SG.7.1.S
-HI.1.0.0.V SG.6.0.S HR.1.0.0.V HE.2.1.1.0.S B.9.1.T BA.7.2.V HR.2.1.0.V BA.9.1.V B.8.0.T AQ.2.1.1.1.T
-SG.7.2.S B.5.1.T HE.2.1.1.1.S B.5.2.T BA.8.0.V BA.5.1.V BA.5.2.V B.4.1.T SG.8.0.S HI.2.1.1.V
-B.6.1.T B.5.0.T BA.4.1.V HR.2.1.1.V BA.6.1.V B.10.2.T B.4.0.T BA.5.0.V BA.10.2.V SG.9.1.S
-SG.5.2.S B.11.2.T B.10.0.T BA.4.0.V BA.11.2.V B.11.1.T SG.5.1.S SG.4.1.S SG.6.1.S BA.10.0.V
-SG.5.0.S BA.11.1.V B.4.2.T BA.4.2.V SG.10.2.S B.10.1.T SG.4.0.S SG.11.2.S B.2.1.T SG.10.0.S
-BA.10.1.V B.11.0.T BA.2.1.V SG.11.1.S SG.4.2.S SG.10.1.S BA.11.0.V SG.2.1.S B.8.1.T SG.11.0.S
-BA.8.1.V SG.8.1.S
-"""
 
 
 def tile_bilinear_edge_decoder_d9_kernel(tc, z_bytes, z_scale, w, x, d_bytes, d_scale, r, b, out):
     nc = tc.nc
-    steps = [(s.split(".")[0], [int(v) for v in s.split(".")[1:-1]], s.split(".")[-1]) for s in ORDER.split()]
-    eng = {}
-    for s in ORDER.split():
-        parts = s.split(".")
-        eng[".".join(parts[:-1])] = parts[-1]
     with ExitStack() as ctx:
         keep = ctx.enter_context(tc.tile_pool(name="keep", bufs=1))
-        zwp = ctx.enter_context(tc.tile_pool(name="zwp", bufs=6))
-        two = ctx.enter_context(tc.tile_pool(name="two", bufs=2))
-        lgp = ctx.enter_context(tc.tile_pool(name="lgp", bufs=14))
-        ps_t = ctx.enter_context(tc.psum_pool(name="ps_t", bufs=2))
-        ps_1 = ctx.enter_context(tc.psum_pool(name="ps_1", bufs=3))
-        ps_2 = ctx.enter_context(tc.psum_pool(name="ps_2", bufs=3))
+        stage = ctx.enter_context(tc.tile_pool(name="stage", bufs=2))
+        turn_banks = ctx.enter_context(tc.psum_pool(name="turn_banks", bufs=2))
+        h_banks = ctx.enter_context(tc.psum_pool(name="h_banks", bufs=3))
+        logit_banks = ctx.enter_context(tc.psum_pool(name="logit_banks", bufs=3))
         ctx.enter_context(tc.manual_schedule())
 
-        zs = keep.tile([P, 12, 8], F32, name="zs")
-        ds = keep.tile([P, 8], F32, name="ds")
-        rt = keep.tile([P, 2, 4], BF16, name="rt")
-        bt = keep.tile([P, N], BF16, name="bt")
-        zb = [keep.tile([P, 4, K], U8, name="zb%d" % c) for c in range(NCH)]
-        xb = [keep.tile([P, 4, F], BF16, name="xb%d" % c) for c in range(NCH)]
-        wr = [[keep.tile([P, 4, 512], BF16, name="wr%d%d" % (h, g)) for g in range(2)] for h in range(2)]
-        db = [keep.tile([P, 4, 512], U8, name="db%d" % h) for h in range(2)]
+        z_codes_in = [keep.tile([P, 2, K], U8, name="z_codes_in%d" % i) for i in range(HALVES)]
+        z_scales_in = keep.tile([P, TILES, 8], F32, name="z_scales_in")
+        x_in = [keep.tile([P, 2, F], BF16, name="x_in%d" % i) for i in range(HALVES)]
+        w_in = [[keep.tile([P, 4, PASS], BF16, name="w_in%d%d" % (h, g)) for g in range(2)] for h in range(2)]
+        d_codes_in = [keep.tile([P, 4, PASS], U8, name="d_codes_in%d" % h) for h in range(2)]
+        d_scale_rows = keep.tile([P, 8], F32, name="d_scale_rows")
+        r_in = keep.tile([P, 8], BF16, name="r_in")
+        bias = keep.tile([P, N], BF16, name="bias")
 
-        drow = keep.tile([P, 8], F32, name="drow")
-        sel = keep.tile([P, P], F32, name="sel")
-        nc.vector.memset(drow[:], 0.0)
-        nc.vector.memset(sel[:], 0.0)
+        z_words = [keep.tile([P, 2, BLOCK], U32, name="z_words%d" % c, align_bytes=256) for c in range(BLOCKS)]
+        z_scales = [keep.tile([P, 2, BLOCK], U8, name="z_scales%d" % c, align_bytes=256) for c in range(BLOCKS)]
+        x_words = [keep.tile([P, HALF], U32, name="x_words%d" % i, align_bytes=256) for i in range(HALVES)]
+        x_scales = [keep.tile([P, HALF], U8, name="x_scales%d" % i, align_bytes=256) for i in range(HALVES)]
+        w_words = [keep.tile([P, 2, PASS], U32, name="w_words%d" % h, align_bytes=256) for h in range(2)]
+        w_scales = [keep.tile([P, 2, PASS], U8, name="w_scales%d" % h, align_bytes=256) for h in range(2)]
+        d_words = [keep.tile([P, PASS], U32, name="d_words%d" % h, align_bytes=256) for h in range(2)]
+        d_scales = [keep.tile([P, PASS], U8, name="d_scales%d" % h, align_bytes=256) for h in range(2)]
+        h_words = [keep.tile([P, 2, HALF], U32, name="h_words%d" % i, align_bytes=256) for i in range(HALVES)]
+        h_scales = [keep.tile([P, 2, HALF], U8, name="h_scales%d" % i, align_bytes=256) for i in range(HALVES)]
+
+        d_scale_cols = keep.tile([P, 8], F32, name="d_scale_cols")
+        r_cols = keep.tile([P, 8], F32, name="r_cols")
+        identity = keep.tile([P, P], F32, name="identity")
+        spread = keep.tile([P, P], F32, name="spread")
+        nc.vector.memset(spread[:], 0.0)
+        nc.scalar.activation(d_scale_rows[:], spread[:, 0:8], ACT.Copy)
         for a in range(4):
-            nc.vector.memset(sel[32 * a:32 * a + 1, 32 * a:32 * a + 32], 1.0)
-        warm = keep.tile([P, 1], F32, name="warm")
-        nc.vector.memset(warm[:], 0.0)
-        nc.scalar.activation(warm[:], warm[:], ACT.Sigmoid)
-        ident = keep.tile([P, P], F32, name="ident")
-        make_identity(nc, ident[:])
-        nc.gpsimd.dma_start(out=rt[:], in_=r.rearrange("(h p t) -> p h t", h=2, p=P))
-        rf = keep.tile([P, 8], F32, name="rf")
-        nc.gpsimd.tensor_copy(rf[:], rt[:].rearrange("p h t -> p (h t)"))
+            nc.vector.memset(spread[32 * a : 32 * a + 1, 32 * a : 32 * a + 32], 1.0)
+        make_identity(nc, identity[:])
+        nc.gpsimd.dma_start(
+            out=r_in[:].rearrange("p (h t) -> p h t", h=2), in_=r.rearrange("(h p t) -> p h t", h=2, p=P)
+        )
+        nc.gpsimd.tensor_copy(r_cols[:], r_in[:])
 
-        for ld in LOADS.split(","):
-            if ld == "zs":
-                nc.sync.dma_start(out=zs[:, 0:4, :], in_=z_scale[0:CH, :].rearrange("(n p) c -> p n c", p=P))
-            elif ld == "zr":
-                nc.sync.dma_start(out=zs[:, 4:12, :], in_=z_scale[CH:N, :].rearrange("(n p) c -> p n c", p=P))
-            elif ld == "dr":
-                nc.sync.dma_start(out=drow[0:P:32, :], in_=d_scale)
-            elif ld == "b":
-                nc.sync.dma_start(out=bt[:], in_=b.partition_broadcast(P))
-            elif ld[0] == "z":
-                c, i = int(ld[1]), int(ld[3])
-                nc.sync.dma_start(out=zb[c][:, 2 * i:2 * i + 2, :], in_=z_bytes[CH * c + 256 * i:CH * c + 256 * i + 256, :].rearrange("(n p) k -> p n k", p=P))
-            elif ld[0] == "x":
-                c, i = int(ld[1]), int(ld[3])
-                nc.sync.dma_start(out=xb[c][:, 2 * i:2 * i + 2, :], in_=x[CH * c + 256 * i:CH * c + 256 * i + 256, :].rearrange("(n p) f -> p n f", p=P))
-            elif ld[0] == "w":
-                h, g = int(ld[1]), int(ld[3])
-                nc.sync.dma_start(out=wr[h][g][:], in_=w[512 * g:512 * g + 512, 512 * h:512 * h + 512].rearrange("(p j) c -> p j c", j=4))
-            else:
-                h = int(ld[1])
-                nc.sync.dma_start(out=db[h][:], in_=d_bytes[:, 512 * h:512 * h + 512].rearrange("(p j) c -> p j c", j=4))
+        def load_z_scales(first, last):
+            nc.sync.dma_start(
+                out=z_scales_in[:, first:last, :],
+                in_=z_scale[first * TILE : last * TILE, :].rearrange("(n p) c -> p n c", p=P),
+            )
 
-        zc = [keep.tile([P, 2, CH], U32, name="zc%d" % c, align_bytes=256) for c in range(NCH)]
-        zsc = [keep.tile([P, 2, CH], U8, name="zsc%d" % c, align_bytes=256) for c in range(NCH)]
-        xc = [keep.tile([P, CH], U32, name="xc%d" % c, align_bytes=256) for c in range(NCH)]
-        xsc = [keep.tile([P, CH], U8, name="xsc%d" % c, align_bytes=256) for c in range(NCH)]
-        wc = [keep.tile([P, 2, 512], U32, name="wc%d" % h, align_bytes=256) for h in range(2)]
-        wsc = [keep.tile([P, 2, 512], U8, name="wsc%d" % h, align_bytes=256) for h in range(2)]
-        dc = [keep.tile([P, 512], U32, name="dc%d" % h, align_bytes=256) for h in range(2)]
-        dsc = [keep.tile([P, 512], U8, name="dsc%d" % h, align_bytes=256) for h in range(2)]
-        hc = [[keep.tile([P, 2, 256], U32, name="hc%d%d" % (c, m), align_bytes=256) for m in range(2)] for c in range(NCH)]
-        hsc = [[keep.tile([P, 2, 256], U8, name="hsc%d%d" % (c, m), align_bytes=256) for m in range(2)] for c in range(NCH)]
-        zt = [keep.tile([P, 2, 2, 1024], BF16, name="zt%d" % c, align_bytes=64) for c in range(NCH)]
-        xt = [keep.tile([P, 2, 1024], BF16, name="xt%d" % c, align_bytes=64) for c in range(NCH)]
-        wt = [keep.tile([P, 2, 2048], BF16, name="wt%d" % h, align_bytes=64) for h in range(2)]
-        dw = [keep.tile([P, 4, 512], BF16, name="dw%d" % h) for h in range(2)]
-        dt = [keep.tile([P, 2048], BF16, name="dt%d" % h, align_bytes=64) for h in range(2)]
-        st = {}
+        def load_z(i):
+            nc.sync.dma_start(
+                out=z_codes_in[i][:], in_=z_bytes[HALF * i : HALF * i + HALF, :].rearrange("(n p) k -> p n k", p=P)
+            )
 
-        def quant(codes, scales, src):
-            nc.vector.quantize_mx(out=codes.bitcast(FP8X4), scales=scales, in_=src)
+        def load_x(i):
+            nc.sync.dma_start(out=x_in[i][:], in_=x[HALF * i : HALF * i + HALF, :].rearrange("(n p) f -> p n f", p=P))
 
-        def copy(e, dst, src):
-            if e == "V":
+        def load_w(h, g):
+            rows, cols = slice(PASS * g, PASS * g + PASS), slice(PASS * h, PASS * h + PASS)
+            nc.sync.dma_start(out=w_in[h][g][:], in_=w[rows, cols].rearrange("(p j) c -> p j c", j=4))
+
+        def load_d(h):
+            cols = slice(PASS * h, PASS * h + PASS)
+            nc.sync.dma_start(out=d_codes_in[h][:], in_=d_bytes[:, cols].rearrange("(p j) c -> p j c", j=4))
+
+        load_z_scales(0, 4)
+        load_z(0)
+        nc.sync.dma_start(out=d_scale_rows[0:P:32, :], in_=d_scale)
+        load_d(0)
+        load_w(0, 0)
+        load_w(0, 1)
+        load_x(0)
+        load_z_scales(4, TILES)
+        load_z(1)
+        load_x(1)
+        load_w(1, 0)
+        load_w(1, 1)
+        load_d(1)
+        for i in (2, 4):
+            load_z(i)
+            load_z(i + 1)
+            load_x(i)
+            load_x(i + 1)
+        nc.sync.dma_start(out=bias[:], in_=b.partition_broadcast(P))
+
+        made = {}
+
+        def copy(engine, dst, src):
+            if engine == "vector":
                 nc.vector.tensor_copy(dst, src)
-            elif e == "S":
-                nc.scalar.copy(dst, src)
             else:
-                nc.gpsimd.tensor_scalar(dst, src, 1.0, 0.0, MULT, ADD)
+                nc.scalar.copy(dst, src)
 
-        def do_ZW(e, n):
-            c, i = n // 4, n % 4
-            zw = zwp.tile([P, K], BF16, name="zw", align_bytes=64)
-            st["zw", n] = zw
+        def quantize(words, scales, values):
+            nc.vector.quantize_mx(out=words.bitcast(FP8X4), scales=scales, in_=values)
+
+        def widen_z(n, engine):
+            wide = stage.tile([P, K], BF16, name="wide", align_bytes=64, bufs=6)
+            made["wide", n] = wide, engine
             for q in range(8):
-                src = zb[c][:, i, P * q:P * q + P].bitcast(FP8)
-                if e == "V":
-                    g, m = q // 4, 32 * (q % 4)
-                    dst = zw[:].rearrange("P (g u p e) -> P g p u e", g=2, u=2, e=2)[:, g, m:m + 32, :, :]
-                    nc.vector.tensor_scalar(dst, src.rearrange("P (p u e) -> P p u e", u=2, e=2), zs[:, n, q:q + 1], None, MULT)
+                k0 = 128 * q
+                codes = z_codes_in[n // 2][:, n % 2, k0 : k0 + 128].bitcast(FP8)
+                scale = z_scales_in[:, n, q : q + 1]
+                if engine == "vector":
+                    sorted_k = wide[:].rearrange("q (g u p e) -> q g p u e", g=2, u=2, e=2)
+                    dst = sorted_k[:, q // 4, 32 * (q % 4) : 32 * (q % 4) + 32, :, :]
+                    nc.vector.tensor_scalar(dst, codes.rearrange("q (p u e) -> q p u e", u=2, e=2), scale, None, MULT)
                 else:
-                    nc.scalar.activation(zw[:, P * q:P * q + P], src, ACT.Copy, scale=zs[:, n, q:q + 1])
+                    nc.scalar.activation(wide[:, k0 : k0 + 128], codes, ACT.Copy, scale=scale)
 
-        def do_ZT(e, n):
-            words = st["zw", n][:].bitcast(F32)
-            bank = ps_t.tile([P, 4, P], F32, name="tbank")
-            st["zp", n] = bank
+        def turn_z(n):
+            wide, engine = made["wide", n]
+            words = wide[:].bitcast(F32)
+            bank = turn_banks.tile([P, 4, TILE], F32, name="turned")
+            made["z turned", n] = bank
             for g in range(2):
                 for u in range(2):
-                    if eng["ZW.%d" % n] == "V":
-                        src = words[:, 256 * g + 128 * u:256 * g + 128 * u + 128]
+                    if engine == "vector":
+                        pairs = words[:, 256 * g + 128 * u : 256 * g + 128 * u + 128]
                     else:
-                        src = words[:, 256 * g + u:256 * g + 256:2]
-                    nc.tensor.transpose(bank[:, 2 * g + u, :], src, ident[:])
+                        pairs = words[:, 256 * g + u : 256 * g + 256 : 2]
+                    nc.tensor.transpose(bank[:, 2 * g + u, :], pairs, identity[:])
 
-        def do_ZC(e, n):
-            c, i = n // 4, n % 4
-            dst = zt[c][:, i // 2, :, :].bitcast(F32).rearrange("p g (r u) -> p g r u", u=2)[:, :, P * (i % 2):P * (i % 2) + P, :]
-            copy(e, dst, st["zp", n][:].rearrange("p (g u) r -> p g r u", g=2))
+        def lay_z(n):
+            i, m = n // 2, n % 2
+            if ("z laid", i) not in made:
+                made["z laid", i] = stage.tile([P, 2, 4 * HALF], BF16, name="z_laid", align_bytes=64, bufs=3)
+            dst = made["z laid", i][:].bitcast(F32).rearrange("p g (n u) -> p g n u", u=2)
+            src = made["z turned", n][:].rearrange("p (g u) n -> p g n u", g=2)
+            nc.scalar.copy(dst[:, :, TILE * m : TILE * m + TILE, :], src)
 
-        def do_ZQ(e, c, m):
+        def quantize_z(i):
+            cols = slice(HALF * (i % 2), HALF * (i % 2) + HALF)
             for g in range(2):
-                quant(zc[c][:, g, 256 * m:256 * m + 256], zsc[c][:, g, 256 * m:256 * m + 256], zt[c][:, m, g, :])
+                quantize(z_words[i // 2][:, g, cols], z_scales[i // 2][:, g, cols], made["z laid", i][:, g, :])
 
-        def do_XT(e, c, m):
-            bank = ps_t.tile([P, 4, P], F32, name="tbank")
-            st["xp", c, m] = bank
-            for i in range(2):
-                words = xb[c][:, 2 * m + i, :].bitcast(F32)
+        def turn_x(i):
+            bank = turn_banks.tile([P, 4, TILE], F32, name="turned")
+            made["x turned", i] = bank
+            for n in range(2):
+                words = x_in[i][:, n, :].bitcast(F32)
                 for u in range(2):
-                    nc.tensor.transpose(bank[:, 2 * i + u, :], words[:, u:256:2], ident[:])
+                    nc.tensor.transpose(bank[:, 2 * n + u, :], words[:, u : F // 2 : 2], identity[:])
 
-        def do_XC(e, c, m):
-            dst = xt[c][:, m, :].bitcast(F32).rearrange("p (i r u) -> p i r u", i=2, u=2)
-            copy(e, dst, st["xp", c, m][:].rearrange("p (i u) r -> p i r u", u=2))
+        def lay_x(i, engine):
+            laid = stage.tile([P, 4 * HALF], BF16, name="x_laid", align_bytes=64, bufs=5)
+            made["x laid", i] = laid
+            dst = laid[:].bitcast(F32).rearrange("p (m n u) -> p m n u", m=2, u=2)
+            copy(engine, dst, made["x turned", i][:].rearrange("p (m u) n -> p m n u", m=2))
 
-        def do_XQ(e, c, m):
-            quant(xc[c][:, 256 * m:256 * m + 256], xsc[c][:, 256 * m:256 * m + 256], xt[c][:, m, :])
+        def quantize_x(i):
+            quantize(x_words[i][:], x_scales[i][:], made["x laid", i][:])
 
-        def do_WI(e, h, g):
-            copy(e, wt[h][:, g, :].rearrange("p (t m j) -> p m t j", t=4, j=4), wr[h][g][:].rearrange("p j (m t) -> p m t j", t=4))
+        def lay_w(h, g, engine):
+            if ("w laid", h) not in made:
+                made["w laid", h] = stage.tile([P, 2, 4 * PASS], BF16, name="w_laid", align_bytes=64)
+            dst = made["w laid", h][:, g, :].rearrange("p (t m j) -> p m t j", t=4, j=4)
+            copy(engine, dst, w_in[h][g][:].rearrange("p j (m t) -> p m t j", t=4))
 
-        def do_WQ(e, h):
-            quant(wc[h][:].rearrange("p g n -> p (g n)"), wsc[h][:].rearrange("p g n -> p (g n)"), wt[h][:].rearrange("p g n -> p (g n)"))
+        def quantize_w(h):
+            quantize(
+                w_words[h][:].rearrange("p g c -> p (g c)"),
+                w_scales[h][:].rearrange("p g c -> p (g c)"),
+                made["w laid", h][:].rearrange("p g v -> p (g v)"),
+            )
 
-        def do_DW(e, h):
-            dst = dw[h][:].rearrange("p j c -> p (j c)")
-            src = db[h][:].rearrange("p j c -> p (j c)").bitcast(FP8)
-            if e == "V":
-                nc.vector.tensor_copy(dst, src)
-            elif e == "S":
-                nc.scalar.copy(dst, src)
-            else:
-                nc.gpsimd.tensor_copy(dst, src)
+        def widen_d(h):
+            wide = stage.tile([P, 4, PASS], BF16, name="d_wide")
+            made["d wide", h] = wide
+            codes = d_codes_in[h][:].rearrange("p j c -> p (j c)").bitcast(FP8)
+            nc.vector.tensor_copy(wide[:].rearrange("p j c -> p (j c)"), codes)
 
-        def do_DS(e, h):
-            if h == 0:
-                sbank = ps_t.tile([P, 4, P], F32, name="tbank")
-                nc.tensor.matmul(sbank[:, 0, 0:8], lhsT=sel[:], rhs=drow[:], start=True, stop=True)
-                copy(e, ds[:], sbank[:, 0, 0:8])
+        def spread_d_scale():
+            bank = logit_banks.tile([P, BLOCK], F32, name="logits")
+            nc.tensor.matmul(bank[:, 0:8], lhsT=spread[:], rhs=d_scale_rows[:], start=True, stop=True)
+            nc.vector.tensor_copy(d_scale_cols[:], bank[:, 0:8])
+
+        def scale_d(h):
+            laid = stage.tile([P, 4 * PASS], BF16, name="d_laid", align_bytes=64)
+            made["d laid", h] = laid
+            dst = laid[:].rearrange("p (t m j) -> p m t j", t=4, j=4)
+            src = made["d wide", h][:].rearrange("p j (m t) -> p m t j", t=4)
             for q in range(4):
-                dst = dt[h][:].rearrange("p (t m j) -> p m t j", t=4, j=4)[:, 32 * q:32 * q + 32, :, :]
-                src = dw[h][:].rearrange("p j (m t) -> p m t j", t=4)[:, 32 * q:32 * q + 32, :, :]
-                sc = ds[:, 4 * h + q:4 * h + q + 1]
-                if e == "V":
-                    nc.vector.tensor_scalar(dst, src, sc, None, MULT)
-                elif e == "S":
-                    nc.scalar.activation(dst, src, ACT.Copy, scale=sc)
-                else:
-                    nc.gpsimd.tensor_scalar(dst, src, sc, 0.0, MULT, ADD)
+                m = slice(32 * q, 32 * q + 32)
+                scale = d_scale_cols[:, 4 * h + q : 4 * h + q + 1]
+                nc.vector.tensor_scalar(dst[:, m, :, :], src[:, m, :, :], scale, None, MULT)
 
-        def do_DQ(e, h):
-            quant(dc[h][:], dsc[h][:], dt[h][:])
+        def quantize_d(h):
+            quantize(d_words[h][:], d_scales[h][:], made["d laid", h][:])
 
-        def do_AQ(e, c, m, h, tp):
-            cols = slice(256 * m, 256 * m + 256)
-            bank = ps_1.tile([P, 2, 256], F32, name="hbank")
-            st["hp", c, m, h, tp] = bank
-            for i in range(2):
-                t = 2 * tp + i
-                s4 = slice(P * t, P * t + P)
+        def project(i, h, s):
+            c, cols = i // 2, slice(HALF * (i % 2), HALF * (i % 2) + HALF)
+            bank = h_banks.tile([P, 2, HALF], F32, name="sums")
+            made["sums", i, h, s] = bank
+            for v in range(2):
+                t = 2 * s + v
+                sorted_cols = slice(128 * t, 128 * t + 128)
                 for g in range(2):
-                    nc.tensor.matmul_mx(out=bank[:, i, :], lhsT=wc[h][:, g, s4].bitcast(FP8X4), lhsT_scale=wsc[h][:, g, s4], rhs=zc[c][:, g, cols].bitcast(FP8X4), rhs_scale=zsc[c][:, g, cols], start=(g == 0), stop=False)
-                nc.tensor.matmul_mx(out=bank[:, i, :], lhsT=dc[h][:, s4].bitcast(FP8X4), lhsT_scale=dsc[h][:, s4], rhs=xc[c][:, cols].bitcast(FP8X4), rhs_scale=xsc[c][:, cols], start=False, stop=True)
+                    nc.tensor.matmul_mx(
+                        out=bank[:, v, :],
+                        lhsT=w_words[h][:, g, sorted_cols].bitcast(FP8X4),
+                        lhsT_scale=w_scales[h][:, g, sorted_cols],
+                        rhs=z_words[c][:, g, cols].bitcast(FP8X4),
+                        rhs_scale=z_scales[c][:, g, cols],
+                        start=(g == 0),
+                        stop=False,
+                    )
+                nc.tensor.matmul_mx(
+                    out=bank[:, v, :],
+                    lhsT=d_words[h][:, sorted_cols].bitcast(FP8X4),
+                    lhsT_scale=d_scales[h][:, sorted_cols],
+                    rhs=x_words[i][:].bitcast(FP8X4),
+                    rhs_scale=x_scales[i][:],
+                    start=False,
+                    stop=True,
+                )
 
-        def do_HE(e, c, m, h, tp):
-            if ("hpl", c, m, h) not in st:
-                hpl = two.tile([P, 4, 256], BF16, name="hpl", bufs=4)
-                st["hpl", c, m, h] = hpl
-            for i in range(2):
-                t = 2 * tp + i
-                dst = st["hpl", c, m, h][:, t, :]
-                src = st["hp", c, m, h, tp][:, i, :]
-                sc = rf[:, 4 * h + t:4 * h + t + 1]
-                if e == "V":
-                    nc.vector.tensor_scalar(dst, src, sc, None, MULT)
-                else:
-                    nc.scalar.activation(dst, src, ACT.Copy, scale=sc)
+        def scale_h(i, h, s):
+            if ("h planes", i, h) not in made:
+                made["h planes", i, h] = stage.tile([P, 4, HALF], BF16, name="h_planes", bufs=4)
+            for v in range(2):
+                t = 2 * s + v
+                factor = r_cols[:, 4 * h + t : 4 * h + t + 1]
+                src = made["sums", i, h, s][:, v, :]
+                nc.scalar.activation(made["h planes", i, h][:, t, :], src, ACT.Copy, scale=factor)
 
-        def do_HI(e, c, m, h):
-            ht = two.tile([P, 256, 4], BF16, name="ht", align_bytes=64, bufs=6)
-            st["ht", c, m, h] = ht
-            copy(e, ht[:], st["hpl", c, m, h][:].rearrange("p t n -> p n t"))
+        def lay_h(i, h):
+            laid = stage.tile([P, HALF, 4], BF16, name="h_laid", align_bytes=64, bufs=6)
+            made["h laid", i, h] = laid
+            nc.vector.tensor_copy(laid[:], made["h planes", i, h][:].rearrange("p t n -> p n t"))
 
-        def do_HR(e, c, m, h):
-            quant(hc[c][m][:, h, :], hsc[c][m][:, h, :], st["ht", c, m, h][:].rearrange("p n t -> p (n t)"))
+        def quantize_h(i, h):
+            quantize(h_words[i][:, h, :], h_scales[i][:, h, :], made["h laid", i, h][:].rearrange("p n t -> p (n t)"))
 
-        def do_B(e, n, c):
-            bank = ps_2.tile([P, CH], F32, name="obank")
-            st["op", n, c] = bank
+        def edge_logits(n, c):
+            bank = logit_banks.tile([P, BLOCK], F32, name="logits")
+            rows = slice(TILE * (n % 2), TILE * (n % 2) + TILE)
             for g in range(2):
-                rows = slice(P * (n % 2), P * (n % 2) + P)
-                hq, hs = hc[n // 4][n % 4 // 2], hsc[n // 4][n % 4 // 2]
-                nc.tensor.matmul_mx(out=bank[:], lhsT=hq[:, g, rows].bitcast(FP8X4), lhsT_scale=hs[:, g, rows], rhs=zc[c][:, g, :].bitcast(FP8X4), rhs_scale=zsc[c][:, g, :], start=(g == 0), stop=(g == 1))
+                nc.tensor.matmul_mx(
+                    out=bank[:],
+                    lhsT=h_words[n // 2][:, g, rows].bitcast(FP8X4),
+                    lhsT_scale=h_scales[n // 2][:, g, rows],
+                    rhs=z_words[c][:, g, :].bitcast(FP8X4),
+                    rhs_scale=z_scales[c][:, g, :],
+                    start=(g == 0),
+                    stop=(g == 1),
+                )
+            edges = stage.tile([P, BLOCK], F32, name="edges", bufs=16)
+            made["edges", n, c] = edges
+            nc.vector.tensor_tensor(edges[:], bank[:], bias[:, BLOCK * c : BLOCK * c + BLOCK], ADD)
 
-        def do_BA(e, n, c):
-            lg = lgp.tile([P, CH], F32, name="lg")
-            st["lg", n, c] = lg
-            nc.vector.tensor_tensor(lg[:], st["op", n, c][:], bt[:, CH * c:CH * c + CH], ADD)
+        def probabilities(n, c):
+            edges = made["edges", n, c]
+            nc.scalar.activation(edges[:], edges[:], ACT.Sigmoid)
+            nc.sync.dma_start(out=out[TILE * n : TILE * n + TILE, BLOCK * c : BLOCK * c + BLOCK], in_=edges[:])
 
-        def do_SG(e, n, c):
-            og = st["lg", n, c]
-            nc.scalar.activation(og[:], og[:], ACT.Sigmoid)
-            nc.sync.dma_start(out=out[P * n:P * n + P, CH * c:CH * c + CH], in_=og[:])
+        widen_z(1, "vector")
+        widen_z(0, "scalar")
+        widen_d(0)
+        turn_z(1)
+        lay_z(1)
+        spread_d_scale()
+        scale_d(0)
+        lay_w(0, 1, "vector")
+        turn_z(0)
+        lay_w(0, 0, "scalar")
+        quantize_d(0)
+        widen_z(3, "vector")
+        turn_x(0)
+        lay_z(0)
+        widen_z(2, "scalar")
+        lay_x(0, "vector")
+        turn_x(1)
+        quantize_w(0)
+        quantize_z(0)
+        lay_x(1, "scalar")
+        turn_z(2)
+        lay_w(1, 0, "scalar")
+        turn_z(3)
+        lay_z(2)
+        quantize_x(0)
+        lay_z(3)
+        project(0, 0, 0)
+        widen_z(4, "scalar")
+        quantize_x(1)
+        project(0, 0, 1)
+        widen_d(1)
+        widen_z(5, "vector")
+        turn_x(2)
+        lay_x(2, "scalar")
+        quantize_z(1)
+        lay_w(1, 1, "vector")
+        scale_d(1)
+        turn_x(3)
+        lay_x(3, "scalar")
+        project(1, 0, 0)
+        quantize_w(1)
+        turn_z(4)
+        scale_h(0, 0, 0)
+        quantize_d(1)
+        scale_h(0, 0, 1)
+        lay_z(4)
+        turn_z(5)
+        project(1, 0, 1)
+        turn_x(5)
+        widen_z(6, "vector")
+        lay_z(5)
+        scale_h(1, 0, 0)
+        lay_x(5, "vector")
+        turn_x(4)
+        scale_h(1, 0, 1)
+        lay_x(4, "scalar")
+        quantize_z(2)
+        quantize_x(2)
+        project(0, 1, 0)
+        widen_z(7, "vector")
+        lay_h(0, 0)
+        scale_h(0, 1, 0)
+        project(0, 1, 1)
+        project(1, 1, 1)
+        project(1, 1, 0)
+        lay_h(1, 0)
+        widen_z(9, "vector")
+        turn_z(6)
+        scale_h(0, 1, 1)
+        lay_h(0, 1)
+        turn_z(7)
+        scale_h(1, 1, 1)
+        widen_z(8, "scalar")
+        scale_h(1, 1, 0)
+        lay_z(7)
+        project(2, 0, 1)
+        project(2, 0, 0)
+        quantize_h(0, 0)
+        lay_z(6)
+        project(2, 1, 0)
+        quantize_x(3)
+        lay_h(1, 1)
+        scale_h(2, 0, 1)
+        quantize_h(0, 1)
+        scale_h(2, 0, 0)
+        quantize_z(3)
+        turn_z(8)
+        widen_z(11, "vector")
+        turn_z(9)
 
-        table = dict(ZW=do_ZW, ZT=do_ZT, ZC=do_ZC, ZQ=do_ZQ, XT=do_XT, XC=do_XC, XQ=do_XQ, WI=do_WI, WQ=do_WQ, DW=do_DW, DS=do_DS, DQ=do_DQ, AQ=do_AQ, HE=do_HE, HI=do_HI, HR=do_HR, B=do_B, BA=do_BA, SG=do_SG)
-        for kind, args, e in steps:
-            table[kind](e, *args)
+        later = []
+
+        def after(blocks, step, *which):
+            later.append([blocks, step, which])
+
+        def advance():
+            due = [entry for entry in later if entry[0] <= 0]
+            rest = [[blocks - 1, step, which] for blocks, step, which in later if blocks > 0]
+            later.clear()
+            later.extend(rest)
+            for blocks, step, which in due:
+                step(*which)
+
+        def next_logits(n, c):
+            advance()
+            edge_logits(n, c)
+            after(2, probabilities, n, c)
+
+        edge_logits(1, 0)
+        lay_z(8)
+        widen_z(10, "scalar")
+        project(2, 1, 1)
+        lay_z(9)
+        quantize_h(1, 0)
+        edge_logits(0, 1)
+        quantize_x(4)
+        turn_z(11)
+        scale_h(2, 1, 1)
+        quantize_h(1, 1)
+        lay_z(11)
+        quantize_x(5)
+        turn_z(10)
+        quantize_z(4)
+        scale_h(2, 1, 0)
+        lay_z(10)
+        edge_logits(0, 0)
+        lay_h(2, 0)
+        quantize_z(5)
+        after(1, probabilities, 1, 0)
+        after(1, lay_h, 2, 1)
+        after(2, probabilities, 0, 1)
+        after(2, quantize_h, 2, 0)
+        after(3, probabilities, 0, 0)
+        after(3, quantize_h, 2, 1)
+
+        waiting = [(1, 1)] + [(n, c) for c in (0, 1) for n in (2, 3)] + [(n, 2) for n in range(4)]
+        waiting += [(n, c) for n in range(4, TILES) for c in range(BLOCKS)]
+        first = 0
+        for number, i in enumerate((3, 4, 5)):
+            for h in range(2):
+                for s in range(2):
+                    project(i, h, s)
+                    after(0, scale_h, i, h, s)
+                    if s == 1:
+                        after(3, lay_h, i, h)
+                        after(5, quantize_h, i, h)
+                    for n, c in waiting[first : first + number + 1]:
+                        next_logits(n, c)
+                    first += number + 1
+                    advance()
+        for n, c in waiting[first:]:
+            next_logits(n, c)
+        while later:
+            advance()

from contextlib import ExitStack

import concourse.mybir as mybir
from concourse.masks import make_identity

F32 = mybir.dt.float32
BF16 = mybir.dt.bfloat16
U32 = mybir.dt.uint32
U8 = mybir.dt.uint8
FP8 = mybir.dt.float8_e4m3fn
FP8X4 = mybir.dt.float8_e4m3fn_x4
MULT = mybir.AluOpType.mult
ADD = mybir.AluOpType.add
ACT = mybir.ActivationFunctionType

N, K, F = 1536, 1024, 512
P = 128
PASS = 512
TILE = 128
HALF = 256
BLOCK = 512
TILES, HALVES, BLOCKS = N // TILE, N // HALF, N // BLOCK
FLOPS = 2 * N * K * K + 2 * N * F * K + 2 * N * N * K


def tile_bilinear_edge_decoder_d9_kernel(tc, z_bytes, z_scale, w, x, d_bytes, d_scale, r, b, out):
    nc = tc.nc
    with ExitStack() as ctx:
        keep = ctx.enter_context(tc.tile_pool(name="keep", bufs=1))
        stage = ctx.enter_context(tc.tile_pool(name="stage", bufs=2))
        turn_banks = ctx.enter_context(tc.psum_pool(name="turn_banks", bufs=2))
        h_banks = ctx.enter_context(tc.psum_pool(name="h_banks", bufs=3))
        logit_banks = ctx.enter_context(tc.psum_pool(name="logit_banks", bufs=3))
        ctx.enter_context(tc.manual_schedule())

        z_codes_in = [keep.tile([P, 2, K], U8, name="z_codes_in%d" % i) for i in range(HALVES)]
        z_scales_in = keep.tile([P, TILES, 8], F32, name="z_scales_in")
        x_in = [keep.tile([P, 2, F], BF16, name="x_in%d" % i) for i in range(HALVES)]
        w_in = [[keep.tile([P, 4, PASS], BF16, name="w_in%d%d" % (h, g)) for g in range(2)] for h in range(2)]
        d_codes_in = [keep.tile([P, 4, PASS], U8, name="d_codes_in%d" % h) for h in range(2)]
        d_scale_rows = keep.tile([P, 8], F32, name="d_scale_rows")
        r_in = keep.tile([P, 8], BF16, name="r_in")
        bias = keep.tile([P, N], BF16, name="bias")

        z_words = [keep.tile([P, 2, BLOCK], U32, name="z_words%d" % c, align_bytes=256) for c in range(BLOCKS)]
        z_scales = [keep.tile([P, 2, BLOCK], U8, name="z_scales%d" % c, align_bytes=256) for c in range(BLOCKS)]
        x_words = [keep.tile([P, HALF], U32, name="x_words%d" % i, align_bytes=256) for i in range(HALVES)]
        x_scales = [keep.tile([P, HALF], U8, name="x_scales%d" % i, align_bytes=256) for i in range(HALVES)]
        w_words = [keep.tile([P, 2, PASS], U32, name="w_words%d" % h, align_bytes=256) for h in range(2)]
        w_scales = [keep.tile([P, 2, PASS], U8, name="w_scales%d" % h, align_bytes=256) for h in range(2)]
        d_words = [keep.tile([P, PASS], U32, name="d_words%d" % h, align_bytes=256) for h in range(2)]
        d_scales = [keep.tile([P, PASS], U8, name="d_scales%d" % h, align_bytes=256) for h in range(2)]
        h_words = [keep.tile([P, 2, HALF], U32, name="h_words%d" % i, align_bytes=256) for i in range(HALVES)]
        h_scales = [keep.tile([P, 2, HALF], U8, name="h_scales%d" % i, align_bytes=256) for i in range(HALVES)]

        d_scale_cols = keep.tile([P, 8], F32, name="d_scale_cols")
        r_cols = keep.tile([P, 8], F32, name="r_cols")
        identity = keep.tile([P, P], F32, name="identity")
        spread = keep.tile([P, P], F32, name="spread")
        nc.vector.memset(spread[:], 0.0)
        nc.scalar.activation(d_scale_rows[:], spread[:, 0:8], ACT.Copy)
        for a in range(4):
            nc.vector.memset(spread[32 * a : 32 * a + 1, 32 * a : 32 * a + 32], 1.0)
        make_identity(nc, identity[:])
        nc.gpsimd.dma_start(
            out=r_in[:].rearrange("p (h t) -> p h t", h=2), in_=r.rearrange("(h p t) -> p h t", h=2, p=P)
        )
        nc.gpsimd.tensor_copy(r_cols[:], r_in[:])

        def load_z_scales(first, last):
            nc.sync.dma_start(
                out=z_scales_in[:, first:last, :],
                in_=z_scale[first * TILE : last * TILE, :].rearrange("(n p) c -> p n c", p=P),
            )

        def load_z(i):
            nc.sync.dma_start(
                out=z_codes_in[i][:], in_=z_bytes[HALF * i : HALF * i + HALF, :].rearrange("(n p) k -> p n k", p=P)
            )

        def load_x(i):
            nc.sync.dma_start(out=x_in[i][:], in_=x[HALF * i : HALF * i + HALF, :].rearrange("(n p) f -> p n f", p=P))

        def load_w(h, g):
            rows, cols = slice(PASS * g, PASS * g + PASS), slice(PASS * h, PASS * h + PASS)
            nc.sync.dma_start(out=w_in[h][g][:], in_=w[rows, cols].rearrange("(p j) c -> p j c", j=4))

        def load_d(h):
            cols = slice(PASS * h, PASS * h + PASS)
            nc.sync.dma_start(out=d_codes_in[h][:], in_=d_bytes[:, cols].rearrange("(p j) c -> p j c", j=4))

        load_z_scales(0, 4)
        load_z(0)
        nc.sync.dma_start(out=d_scale_rows[0:P:32, :], in_=d_scale)
        load_d(0)
        load_w(0, 0)
        load_w(0, 1)
        load_x(0)
        load_z_scales(4, TILES)
        load_z(1)
        load_x(1)
        load_w(1, 0)
        load_w(1, 1)
        load_d(1)
        for i in (2, 4):
            load_z(i)
            load_z(i + 1)
            load_x(i)
            load_x(i + 1)
        nc.sync.dma_start(out=bias[:], in_=b.partition_broadcast(P))

        made = {}

        def copy(engine, dst, src):
            if engine == "vector":
                nc.vector.tensor_copy(dst, src)
            else:
                nc.scalar.copy(dst, src)

        def quantize(words, scales, values):
            nc.vector.quantize_mx(out=words.bitcast(FP8X4), scales=scales, in_=values)

        def widen_z(n, engine):
            wide = stage.tile([P, K], BF16, name="wide", align_bytes=64, bufs=6)
            made["wide", n] = wide, engine
            for q in range(8):
                k0 = 128 * q
                codes = z_codes_in[n // 2][:, n % 2, k0 : k0 + 128].bitcast(FP8)
                scale = z_scales_in[:, n, q : q + 1]
                if engine == "vector":
                    sorted_k = wide[:].rearrange("q (g u p e) -> q g p u e", g=2, u=2, e=2)
                    dst = sorted_k[:, q // 4, 32 * (q % 4) : 32 * (q % 4) + 32, :, :]
                    nc.vector.tensor_scalar(dst, codes.rearrange("q (p u e) -> q p u e", u=2, e=2), scale, None, MULT)
                else:
                    nc.scalar.activation(wide[:, k0 : k0 + 128], codes, ACT.Copy, scale=scale)

        def turn_z(n):
            wide, engine = made["wide", n]
            words = wide[:].bitcast(F32)
            bank = turn_banks.tile([P, 4, TILE], F32, name="turned")
            made["z turned", n] = bank
            for g in range(2):
                for u in range(2):
                    if engine == "vector":
                        pairs = words[:, 256 * g + 128 * u : 256 * g + 128 * u + 128]
                    else:
                        pairs = words[:, 256 * g + u : 256 * g + 256 : 2]
                    nc.tensor.transpose(bank[:, 2 * g + u, :], pairs, identity[:])

        def lay_z(n):
            i, m = n // 2, n % 2
            if ("z laid", i) not in made:
                made["z laid", i] = stage.tile([P, 2, 4 * HALF], BF16, name="z_laid", align_bytes=64, bufs=3)
            dst = made["z laid", i][:].bitcast(F32).rearrange("p g (n u) -> p g n u", u=2)
            src = made["z turned", n][:].rearrange("p (g u) n -> p g n u", g=2)
            nc.scalar.copy(dst[:, :, TILE * m : TILE * m + TILE, :], src)

        def quantize_z(i):
            cols = slice(HALF * (i % 2), HALF * (i % 2) + HALF)
            for g in range(2):
                quantize(z_words[i // 2][:, g, cols], z_scales[i // 2][:, g, cols], made["z laid", i][:, g, :])

        def turn_x(i):
            bank = turn_banks.tile([P, 4, TILE], F32, name="turned")
            made["x turned", i] = bank
            for n in range(2):
                words = x_in[i][:, n, :].bitcast(F32)
                for u in range(2):
                    nc.tensor.transpose(bank[:, 2 * n + u, :], words[:, u : F // 2 : 2], identity[:])

        def lay_x(i, engine):
            laid = stage.tile([P, 4 * HALF], BF16, name="x_laid", align_bytes=64, bufs=5)
            made["x laid", i] = laid
            dst = laid[:].bitcast(F32).rearrange("p (m n u) -> p m n u", m=2, u=2)
            copy(engine, dst, made["x turned", i][:].rearrange("p (m u) n -> p m n u", m=2))

        def quantize_x(i):
            quantize(x_words[i][:], x_scales[i][:], made["x laid", i][:])

        def lay_w(h, g, engine):
            if ("w laid", h) not in made:
                made["w laid", h] = stage.tile([P, 2, 4 * PASS], BF16, name="w_laid", align_bytes=64)
            dst = made["w laid", h][:, g, :].rearrange("p (t m j) -> p m t j", t=4, j=4)
            copy(engine, dst, w_in[h][g][:].rearrange("p j (m t) -> p m t j", t=4))

        def quantize_w(h):
            quantize(
                w_words[h][:].rearrange("p g c -> p (g c)"),
                w_scales[h][:].rearrange("p g c -> p (g c)"),
                made["w laid", h][:].rearrange("p g v -> p (g v)"),
            )

        def widen_d(h):
            wide = stage.tile([P, 4, PASS], BF16, name="d_wide")
            made["d wide", h] = wide
            codes = d_codes_in[h][:].rearrange("p j c -> p (j c)").bitcast(FP8)
            nc.vector.tensor_copy(wide[:].rearrange("p j c -> p (j c)"), codes)

        def spread_d_scale():
            bank = logit_banks.tile([P, BLOCK], F32, name="logits")
            nc.tensor.matmul(bank[:, 0:8], lhsT=spread[:], rhs=d_scale_rows[:], start=True, stop=True)
            nc.vector.tensor_copy(d_scale_cols[:], bank[:, 0:8])

        def scale_d(h):
            laid = stage.tile([P, 4 * PASS], BF16, name="d_laid", align_bytes=64)
            made["d laid", h] = laid
            dst = laid[:].rearrange("p (t m j) -> p m t j", t=4, j=4)
            src = made["d wide", h][:].rearrange("p j (m t) -> p m t j", t=4)
            for q in range(4):
                m = slice(32 * q, 32 * q + 32)
                scale = d_scale_cols[:, 4 * h + q : 4 * h + q + 1]
                nc.vector.tensor_scalar(dst[:, m, :, :], src[:, m, :, :], scale, None, MULT)

        def quantize_d(h):
            quantize(d_words[h][:], d_scales[h][:], made["d laid", h][:])

        def project(i, h, s):
            c, cols = i // 2, slice(HALF * (i % 2), HALF * (i % 2) + HALF)
            bank = h_banks.tile([P, 2, HALF], F32, name="sums")
            made["sums", i, h, s] = bank
            for v in range(2):
                t = 2 * s + v
                sorted_cols = slice(128 * t, 128 * t + 128)
                for g in range(2):
                    nc.tensor.matmul_mx(
                        out=bank[:, v, :],
                        lhsT=w_words[h][:, g, sorted_cols].bitcast(FP8X4),
                        lhsT_scale=w_scales[h][:, g, sorted_cols],
                        rhs=z_words[c][:, g, cols].bitcast(FP8X4),
                        rhs_scale=z_scales[c][:, g, cols],
                        start=(g == 0),
                        stop=False,
                    )
                nc.tensor.matmul_mx(
                    out=bank[:, v, :],
                    lhsT=d_words[h][:, sorted_cols].bitcast(FP8X4),
                    lhsT_scale=d_scales[h][:, sorted_cols],
                    rhs=x_words[i][:].bitcast(FP8X4),
                    rhs_scale=x_scales[i][:],
                    start=False,
                    stop=True,
                )

        def scale_h(i, h, s):
            if ("h planes", i, h) not in made:
                made["h planes", i, h] = stage.tile([P, 4, HALF], BF16, name="h_planes", bufs=4)
            for v in range(2):
                t = 2 * s + v
                factor = r_cols[:, 4 * h + t : 4 * h + t + 1]
                src = made["sums", i, h, s][:, v, :]
                nc.scalar.activation(made["h planes", i, h][:, t, :], src, ACT.Copy, scale=factor)

        def lay_h(i, h):
            laid = stage.tile([P, HALF, 4], BF16, name="h_laid", align_bytes=64, bufs=6)
            made["h laid", i, h] = laid
            nc.vector.tensor_copy(laid[:], made["h planes", i, h][:].rearrange("p t n -> p n t"))

        def quantize_h(i, h):
            quantize(h_words[i][:, h, :], h_scales[i][:, h, :], made["h laid", i, h][:].rearrange("p n t -> p (n t)"))

        def edge_logits(n, c):
            bank = logit_banks.tile([P, BLOCK], F32, name="logits")
            rows = slice(TILE * (n % 2), TILE * (n % 2) + TILE)
            for g in range(2):
                nc.tensor.matmul_mx(
                    out=bank[:],
                    lhsT=h_words[n // 2][:, g, rows].bitcast(FP8X4),
                    lhsT_scale=h_scales[n // 2][:, g, rows],
                    rhs=z_words[c][:, g, :].bitcast(FP8X4),
                    rhs_scale=z_scales[c][:, g, :],
                    start=(g == 0),
                    stop=(g == 1),
                )
            edges = stage.tile([P, BLOCK], F32, name="edges", bufs=16)
            made["edges", n, c] = edges
            nc.vector.tensor_tensor(edges[:], bank[:], bias[:, BLOCK * c : BLOCK * c + BLOCK], ADD)

        def probabilities(n, c):
            edges = made["edges", n, c]
            nc.scalar.activation(edges[:], edges[:], ACT.Sigmoid)
            nc.sync.dma_start(out=out[TILE * n : TILE * n + TILE, BLOCK * c : BLOCK * c + BLOCK], in_=edges[:])

        widen_z(1, "vector")
        widen_z(0, "scalar")
        widen_d(0)
        turn_z(1)
        lay_z(1)
        spread_d_scale()
        scale_d(0)
        lay_w(0, 1, "vector")
        turn_z(0)
        lay_w(0, 0, "scalar")
        quantize_d(0)
        widen_z(3, "vector")
        turn_x(0)
        lay_z(0)
        widen_z(2, "scalar")
        lay_x(0, "vector")
        turn_x(1)
        quantize_w(0)
        quantize_z(0)
        lay_x(1, "scalar")
        turn_z(2)
        lay_w(1, 0, "scalar")
        turn_z(3)
        lay_z(2)
        quantize_x(0)
        lay_z(3)
        project(0, 0, 0)
        widen_z(4, "scalar")
        quantize_x(1)
        project(0, 0, 1)
        widen_d(1)
        widen_z(5, "vector")
        turn_x(2)
        lay_x(2, "scalar")
        quantize_z(1)
        lay_w(1, 1, "vector")
        scale_d(1)
        turn_x(3)
        lay_x(3, "scalar")
        project(1, 0, 0)
        quantize_w(1)
        turn_z(4)
        scale_h(0, 0, 0)
        quantize_d(1)
        scale_h(0, 0, 1)
        lay_z(4)
        turn_z(5)
        project(1, 0, 1)
        turn_x(5)
        widen_z(6, "vector")
        lay_z(5)
        scale_h(1, 0, 0)
        lay_x(5, "vector")
        turn_x(4)
        scale_h(1, 0, 1)
        lay_x(4, "scalar")
        quantize_z(2)
        quantize_x(2)
        project(0, 1, 0)
        widen_z(7, "vector")
        lay_h(0, 0)
        scale_h(0, 1, 0)
        project(0, 1, 1)
        project(1, 1, 1)
        project(1, 1, 0)
        lay_h(1, 0)
        widen_z(9, "vector")
        turn_z(6)
        scale_h(0, 1, 1)
        lay_h(0, 1)
        turn_z(7)
        scale_h(1, 1, 1)
        widen_z(8, "scalar")
        scale_h(1, 1, 0)
        lay_z(7)
        project(2, 0, 1)
        project(2, 0, 0)
        quantize_h(0, 0)
        lay_z(6)
        project(2, 1, 0)
        quantize_x(3)
        lay_h(1, 1)
        scale_h(2, 0, 1)
        quantize_h(0, 1)
        scale_h(2, 0, 0)
        quantize_z(3)
        turn_z(8)
        widen_z(11, "vector")
        turn_z(9)

        later = []

        def after(blocks, step, *which):
            later.append([blocks, step, which])

        def advance():
            due = [entry for entry in later if entry[0] <= 0]
            rest = [[blocks - 1, step, which] for blocks, step, which in later if blocks > 0]
            later.clear()
            later.extend(rest)
            for blocks, step, which in due:
                step(*which)

        def next_logits(n, c):
            advance()
            edge_logits(n, c)
            after(2, probabilities, n, c)

        edge_logits(1, 0)
        lay_z(8)
        widen_z(10, "scalar")
        project(2, 1, 1)
        lay_z(9)
        quantize_h(1, 0)
        edge_logits(0, 1)
        quantize_x(4)
        turn_z(11)
        scale_h(2, 1, 1)
        quantize_h(1, 1)
        lay_z(11)
        quantize_x(5)
        turn_z(10)
        quantize_z(4)
        scale_h(2, 1, 0)
        lay_z(10)
        edge_logits(0, 0)
        lay_h(2, 0)
        quantize_z(5)
        after(1, probabilities, 1, 0)
        after(1, lay_h, 2, 1)
        after(2, probabilities, 0, 1)
        after(2, quantize_h, 2, 0)
        after(3, probabilities, 0, 0)
        after(3, quantize_h, 2, 1)

        waiting = [(1, 1)] + [(n, c) for c in (0, 1) for n in (2, 3)] + [(n, 2) for n in range(4)]
        waiting += [(n, c) for n in range(4, TILES) for c in range(BLOCKS)]
        first = 0
        for number, i in enumerate((3, 4, 5)):
            for h in range(2):
                for s in range(2):
                    project(i, h, s)
                    after(0, scale_h, i, h, s)
                    if s == 1:
                        after(3, lay_h, i, h)
                        after(5, quantize_h, i, h)
                    for n, c in waiting[first : first + number + 1]:
                        next_logits(n, c)
                    first += number + 1
                    advance()
        for n, c in waiting[first:]:
            next_logits(n, c)
        while later:
            advance()
